import numpy as np, ml_dtypes
CORES = [36,164,52,180,100,228,116,244]
N = 8
BF = ml_dtypes.bfloat16
def gentries(a):
    return np.ascontiguousarray(a.reshape(8, 16, -1).transpose(0, 2, 1)).reshape(8, -1)
def gtable(e):
    e = np.asarray(e); return np.ascontiguousarray(e.reshape(8, -1, 16).transpose(0, 2, 1)).reshape(128, -1).astype(np.int32)
W, L, RO, PE, ES, LAST = 4096, 192, 3, 3, 4, 1
def names(rng): return rng.integers(0, W, (N, 8, L, 16))
def pack(x, s, z):
    return {"cont": np.ascontiguousarray(np.reshape(x, (N, 128, W))).astype(np.float32).astype(BF),
            "enz": np.stack([gtable(a.reshape(8, -1)) for a in s]), "subs": np.stack([gtable(a.reshape(8, -1)) for a in z])}
def setup_inputs(rng):
    x = np.where(rng.random((N, 8, 1, W)) < 0.3, 51 * rng.integers(0, 6, (N, 8, 16, W)), rng.integers(0, 256, (N, 8, 16, W)))
    s, z = names(rng), names(rng); u = rng.random((N, 8, L, 1))
    z = np.where((u < 0.15) & (rng.random(z.shape) < 0.3), s[..., 15:], z)
    z = np.where((u > 0.9) & (rng.random(z.shape) < 0.5), z[..., 7:8], z)
    return pack(x, s, z)
def setup_inputs_spread(rng):
    x = np.minimum((np.exp2(3 + 5.5 * rng.random((N, 8, 1, W))) * rng.random((N, 8, 16, W))).astype(np.int64), 255)
    e = rng.choice(np.array([1.0, 1.5, 2.0, 3.0, 4.0]), (N, 8, 1, 1))
    s = np.minimum((W * rng.random((N, 8, L, 16)) ** e).astype(np.int64), W - 1)
    z = W - 1 - np.minimum((W * rng.random((N, 8, L, 16)) ** e).astype(np.int64), W - 1)
    return pack(x, s, z)
def setup_inputs_ends(rng):
    x = 255 * (rng.random((N, 8, 16, W)) < rng.choice(np.array([0.0, 0.1, 0.3, 0.5, 0.7, 0.9, 1.0]), (N, 8, 1, W)))
    near = (np.arange(16)[:, None] == rng.integers(0, 16, (N, 8, 1, W))) & (rng.random((N, 8, 1, W)) < 0.3)
    x = np.where(near, np.where(x == 0, 1, 254), x)
    m = np.stack([np.concatenate([rng.permutation(np.array([0, 10, 6, 8, 7, 9, 12])), np.array([16])]) for q in range(N)])
    top = np.argsort(rng.random((N, 8, 16)), axis=-1) < m[..., None]
    x[..., W - 1] = np.where(top, 255, 0); x[..., 0] = np.where(top, 0, 255)
    x[:, 7, :, W - 2] = 255; x[:, 7, 15, W - 2] = 254; x[:, 7, :, 1] = 0; x[:, 7, 0, 1] = 1
    x[:, 7, :, W - 3] = 255; x[:, 7, 14:, W - 3] = 254
    sz = []
    for i in range(2):
        fr = rng.choice(np.array([1.0, 0.6]), (N, 8, L, 1))
        sz.append(np.where(rng.random((N, 8, L, 16)) < fr, (W - 1) * rng.integers(0, 2, (N, 8, L, 16)), names(rng)))
    s, z = sz; alt = np.where(np.arange(16) & 1 == 1, W - 1, 0)
    for a, b, c in ((L - 1, L - 2, L - 3), (0, 1, 2)):
        s[:, 7, a] = W - 1 - alt; z[:, 7, a] = W - 1; z[:, 7, a, 9] = W - 2; z[:, 7, a, 15] = W - 2
        s[:, 7, b] = alt; z[:, 7, b] = 0
        s[:, 7, c] = alt; z[:, 7, c] = W - 1
        z[:, 7, c, 5] = W - 31
    for i, (p1, p2) in enumerate(((6, 11), (1, 14), (0, 15))):
        for a in (L - 4 - i, 3 + i):
            s[:, 7, a] = W - 1 - alt; z[:, 7, a] = W - 1; z[:, 7, a, p1] = W - 2; z[:, 7, a, p2] = W - 3
    return pack(x, s, z)
def setup_inputs_corners(rng):
    B = W // 16; kind = rng.integers(0, 7, (N, 8, B))
    for q in range(N):
        g = rng.permutation(8); kind[q, g[0]] = 0; kind[q, g[1]] = 3
    opts = ([0, 2, 4], [0, 2, 4], [5, 7, 9, 11], [6, 7, 8, 9], [10, 11, 12, 13], [5, 6, 7, 9, 10], list(range(17)))
    cs = np.zeros((N, 8, B, 16), np.int64)
    for i, o in enumerate(opts): cs = np.where(kind[..., None] == i, rng.choice(np.array(o), cs.shape), cs)
    cs[..., 0] = np.where(kind == 1, rng.choice(np.array([1, 3, 5]), kind.shape), cs[..., 0])
    down = (np.argsort(rng.random((N, 8, B, 16, 16)), axis=-1) < cs[..., None]).transpose(0, 1, 2, 4, 3).copy()
    down[..., 0] &= ~np.all(down, axis=-1)
    st = rng.integers(1, 17, down.shape); v = np.zeros(down.shape, np.int64); cur = np.full(down.shape[:-1], 255)
    for k in range(32):
        v[..., k & 15] = cur; cur = np.where(down[..., k & 15], cur - st[..., k & 15], 255)
    x = np.ascontiguousarray(v.transpose(0, 1, 3, 2, 4)).reshape(N, 8, 16, W)
    blk = np.concatenate([np.argsort(rng.random((N, 8, B)), axis=-1) for i in range(2)], axis=-1)[..., :L]
    rot = np.where(np.arange(L) < B, 0, rng.integers(0, 16, (N, 8, L)))
    s = 16 * blk[..., None] + ((np.arange(16) + rot[..., None]) & 15)
    inv = np.argsort(rng.random((N, 8, W)), axis=-1); new = np.argsort(inv, axis=-1)
    x = np.take_along_axis(x, inv[:, :, None], 3); s = np.take_along_axis(new, s.reshape(N, 8, -1), 2).reshape(N, 8, L, 16)
    one = rng.choice(np.array([0, W - 1, W // 2, 5]), (N, 8, L, 1)); s = np.where(rng.random((N, 8, L, 1)) < 0.1, one, s)
    z = names(rng); zk = rng.integers(0, 7, (N, 8, L, 1)); p = np.arange(16); own = s[..., 15:]
    z = np.where((zk == 1) & (p == 15), own, z); z = np.where((zk == 2) & ((p == 0) | (p == 15)), own, z)
    z = np.where(zk == 3, own, z); z = np.where(zk == 4, s, z)
    z = np.where(zk == 5, (W - 1) * rng.integers(0, 2, z.shape), z); z = np.where((zk == 6) & (p == rng.integers(0, 16, zk.shape)), own, z)
    return pack(x, s, z)
def setup_inputs_ties(rng):
    lev = np.array([[0, 1, 254, 255], [3, 4, 5, 250]])[np.arange(8) & 1]
    x = np.take_along_axis(np.broadcast_to(lev[None], (N, 8, 4)), rng.integers(0, 4, (N, 8, 16 * W)), 2).reshape(N, 8, 16, W)
    pool = rng.integers(0, W, (N, 8, 24)); pool[..., 0] = 0; pool[..., 1] = W - 1
    s = np.take_along_axis(pool, rng.integers(0, 24, (N, 8, L * 16)), 2).reshape(N, 8, L, 16)
    z = np.take_along_axis(pool, rng.integers(0, 24, (N, 8, L * 16)), 2).reshape(N, 8, L, 16)
    u = rng.random((N, 8, L, 1)); z = np.where(u < 0.2, s, z); z = np.where(u > 0.85, z[..., 3:4], z)
    return pack(x, s, z)
def setup_inputs_full(rng):
    B = W // 16; kind = np.stack([rng.permutation(np.array([0, 0, 0, 1, 1, 2, 2, 2])) for q in range(N)]); kind[0, 7] = 1; kind[N - 1, 7] = 0
    k4 = kind[:, :, None, None]
    cs = np.where(k4 == 0, rng.choice(np.array([10, 12, 14]), (N, 8, B, 16)), rng.integers(6, 16, (N, 8, B, 16)))
    cs[..., 0] += ((kind[:, :, None] == 0) & (rng.random((N, 8, B)) < 0.5)).astype(np.int64)
    t1 = np.argsort(rng.random((N, 8, B, 16)), axis=-1); t2 = np.argsort(rng.random((N, 8, B, 16)), axis=-1)
    down = ((t1[..., :, None] + t2[..., None, :]) & 15) < cs[..., None, :]
    st = rng.integers(1, 17, down.shape); v = np.zeros(down.shape, np.int64); cur = np.full(down.shape[:-1], 255)
    for k in range(32):
        v[..., k & 15] = cur; cur = np.where(down[..., k & 15], cur - st[..., k & 15], 255)
    x = np.ascontiguousarray(v.transpose(0, 1, 3, 2, 4)).reshape(N, 8, 16, W)
    blk = np.concatenate([np.argsort(rng.random((N, 8, B)), axis=-1) for i in range(2)], axis=-1)[..., :L]
    s = 16 * blk[..., None] + np.arange(16)
    inv = np.argsort(rng.random((N, 8, W)), axis=-1); new = np.argsort(inv, axis=-1)
    x = np.take_along_axis(x, inv[:, :, None], 3); s = np.take_along_axis(new, s.reshape(N, 8, -1), 2).reshape(N, 8, L, 16)
    hi = np.arange(W - 96, W); ok = ((hi[:, None] * np.arange(W) >> 5) & (W - 1)) + hi[:, None] + 77 == 2 * W
    made = np.where(np.any(ok, axis=1), np.argmax(ok, axis=1), -1); y = W - 32 + ((-((hi & 31) ** 7)) & 31)
    mate = np.full(W, -1); mate[W - 96:] = np.where(((hi & 1) == 1) & (hi * (y + 32) > 2 ** 24), y, made)
    zu = np.where(mate[s] >= 0, mate[s], names(rng)); zu[..., 0] = s[..., 15]
    way = 1 - 2 * (np.take_along_axis(cs[..., 0], blk, 2) & 1)
    p = (rng.integers(0, 16, (N, 8, L, 1)) + way[..., None] * np.arange(16)) & 15
    z = np.take_along_axis(zu, np.argsort(p, axis=-1), 3)
    z = np.where(rng.random((N, 8, L, 1)) < 0.75, z, names(rng))
    pm = np.argsort(rng.random((N, 8, W)), axis=-1); cl = (np.argsort(pm, axis=-1) >> 9)[:, :, None]
    few = rng.integers(0, 4, (N, 8, 16, W)); x2 = rng.integers(0, 256, (N, 8, 16, W)); x2 = np.where(cl == 0, few, x2)
    for i, b in ((1, 134), (2, 198), (3, 255)): x2 = np.where(cl == i, b - few, x2)
    s2 = names(rng); s2[..., 15] = np.take_along_axis(pm, rng.integers(0, 512, (N, 8, L)), 2)
    zi = 512 * rng.integers(1, 4, (N, 8, L, 1)) + rng.integers(0, 512, (N, 8, L, 16))
    z2 = np.take_along_axis(pm, zi.reshape(N, 8, -1), 2).reshape(N, 8, L, 16)
    return pack(np.where(k4 == 2, x2, x), np.where(k4 == 2, s2, s), np.where(k4 == 2, z2, z))
def check_inputs(d):
    bad = []
    c = np.asarray(d["cont"]).astype(np.float32)
    if not np.all((c >= 0) & (c <= 255)): bad.append("range of cont")
    elif not np.all(c == np.floor(c)): bad.append("whole numbers in cont")
    for k in ("enz", "subs"):
        if np.min(d[k]) < 0 or np.max(d[k]) > W - 1: bad.append("range of " + k)
    return bad
def edit(x, s, z, a, t):
    v = np.take_along_axis(x, s.reshape(8, 1, -1), 2).reshape(8, 16, L, 16)
    y = np.take_along_axis(x, z.reshape(8, 1, -1), 2).reshape(8, 16, L, 16)
    c = np.sum((v > np.roll(v, -1, axis=3)).astype(np.int64), axis=1)
    dist = np.sum(np.abs(y - v[..., 15:16]).astype(np.int64), axis=1)
    step = 1 - 2 * (np.add.accumulate(c, axis=2) & 1); step[..., 0] = np.argmin(dist, axis=2)
    pos = np.add.accumulate(step, axis=2) & 15
    hit = pos[:, :, None, :] == np.arange(16)[:, None]
    e = 15 - np.argmax(hit[..., ::-1], axis=3) if LAST else np.argmax(hit, axis=3)
    has = np.any(hit, axis=3); ce = np.take_along_axis(c, e, 2); se = np.take_along_axis(s, e, 2)
    gone = has & (ce <= 5 + (a & 1)[..., None])
    new = np.where(has, np.where(ce <= 9, se, ((se * z >> 5) + se + 77 * t) & (W - 1)), z)
    n = np.sum(gone.astype(np.int64), axis=2); i = np.arange(16) - (16 - n)[..., None]
    kept = np.take_along_axis(new, np.argsort(gone, axis=2, kind="stable"), 2)
    return np.where(i < 0, kept, np.take_along_axis(s, np.maximum(i, 0), 2)), n
def reference(cont, enz, subs):
    x = cont.astype(np.float32).astype(np.int16).reshape(N, 8, 16, W)
    s = np.stack([gentries(a) for a in enz]).astype(np.int64).reshape(N, 8, L, 16)
    z = np.stack([gentries(a) for a in subs]).astype(np.int64).reshape(N, 8, L, 16)
    dels = np.zeros((N, 8, L), np.int64)
    for t in range(1, RO + 1):
        both = [edit(x[r], s[r], z[r], dels[r], t) for r in range(N)]
        dels = np.stack([b[1] for b in both])
        z = np.roll(s, ES, axis=0)
        s = np.roll(np.stack([b[0] for b in both]), PE, axis=0)
    return {"yenz": np.stack([gtable(a.reshape(8, -1)) for a in s]).astype(np.float32), "ysub": np.stack([gtable(a.reshape(8, -1)) for a in z]).astype(np.float32)}

@@ -1,0 +1,431 @@
+from concourse.bass import DstId, RemoteDMATransfer
+from concourse.mybir import dt, AluOpType as A, ActivationFunctionType as F
+
+H = 2
+NL = 12 // H
+W, W17 = 16 * NL, 17 * NL
+NV = 16 * W
+RP = 8 if NL <= 4 else 4
+NP, PC = 16 // RP, RP * W
+R = 3
+CY, VO, SO, PCY = 0.83, 50.0, 65.0, 0.42
+LATE, HOLD, AHEAD, PASSES, WAKE, RLAT = 100, 400.0, 0.8, 4, 60.0, 2500.0
+BIG = 1.0e9
+CKS = 4 if NL <= 4 else 2
+NDIFF = 4
+
+IDENT = (("ip", 1.0, "bfloat16"), ("im", -1.0, "bfloat16"), ("i16th", 1.0 / 16, "bfloat16"), ("i2048", 2048.0, "bfloat16"),
+         ("i16", 16.0, "bfloat16"), ("i32", 32.0, "bfloat16"), ("i4", 4.0, "bfloat16"), ("i8192", 8192.0, "bfloat16"),
+         ("im256", -256.0, "bfloat16"), ("iph", 1.0, "float16"), ("i127h", 127.0, "float16"))
+SCRATCH = {
+    "ct": ("sbuf", [128, 4096], "bfloat16"),
+    "en": ("sbuf", [128, 192], "int32"), "su": ("sbuf", [128, 192], "int32"),
+    "one": ("sbuf", [128, 128], "float32"), "idf": ("sbuf", [128, 128], "float32"),
+    "g8a": ("sbuf", [128, 8], "float32"), "g8b": ("sbuf", [128, 8], "float32"), "g8c": ("sbuf", [128, 8], "float32"),
+    "pid": ("sbuf", [128, 1], "int32"), "pbit": ("sbuf", [128, 1], "int32"),
+    "modd": ("sbuf", [128, 1], "float32"), "meven": ("sbuf", [128, 1], "float32"),
+    "selc": ("sbuf", [128, 160], "bfloat16"), "seld": ("sbuf", [128, 160], "bfloat16"),
+    "kc8": ("sbuf", [128, W], "bfloat16"), "krow": ("sbuf", [128, W], "bfloat16"),
+    "kw": ("sbuf", [128, W17], "bfloat16"), "tg17": ("sbuf", [128, W17], "float32"),
+    "kkeep": ("sbuf", [128, W], "bfloat16"), "kfill": ("sbuf", [128, W], "bfloat16"),
+    "mk17": ("sbuf", [128, W17], "float32"), "rk17": ("sbuf", [128, W17], "float32"),
+    "rm17": ("sbuf", [128, W17], "float32"), "rn17": ("sbuf", [128, W17], "float32"),
+    "mk16": ("sbuf", [128, W], "float32"), "rm16": ("sbuf", [128, W], "float32"),
+    "m0l": ("sbuf", [128, H, W], "uint16"), "ls2": ("sbuf", [128, H, W], "uint16"), "lsn2": ("sbuf", [128, 12, 16], "int32"),
+    "nme": ("sbuf", [128, 12, 16], "int32"), "nms": ("sbuf", [128, 12, 16], "int32"),
+    "pck": ("psum", [128, CKS, 2, 16, 16 // CKS], "float32"),
+    "pe0": ("psum", [128, 8, 64], "float32"), "pe1": ("psum", [128, 8, 64], "float32"),
+    "pw": ("psum", [128, 2 * CKS, 256 // CKS], "float32"),
+}
+for _q in range(NDIFF):
+    SCRATCH["pd%d" % _q] = ("psum", [128, 512], "float32")
+for _n, _v, _d in IDENT:
+    SCRATCH[_n] = ("sbuf", [128, 128], _d)
+for _k in ("e", "s"):
+    SCRATCH["xm" + _k] = ("sbuf", [128, 12, 2, 16], "float32")
+    SCRATCH["xt" + _k] = ("sbuf", [128, 12, 2, 16], "float32")
+for _n, _s, _d in (
+        ("v", [NV], "bfloat16"), ("y", [NV], "bfloat16"), ("sg", [NV], "bfloat16"), ("ab", [NV], "bfloat16"), ("v15", [W], "bfloat16"),
+        ("x17", [2, W17], "float32"), ("km", [W17], "int32"), ("cc", [W17], "int32"), ("par", [W17], "int32"),
+        ("st", [W17], "int32"), ("pb", [W17], "int32"), ("od", [W17], "bfloat16"), ("pos", [W17], "bfloat16"),
+        ("g1", [W17], "bfloat16"), ("g2", [W17], "bfloat16"), ("mx", [W17 + 4], "bfloat16"), ("mn", [W17 + 4], "bfloat16"),
+        ("a17", [NL, 17], "int32"), ("d1", [W17], "float32"), ("u", [W17], "bfloat16"), ("w", [W17], "bfloat16"),
+        ("s2", [2, NL, 16], "int32"), ("q1", [2, NL, 16], "float32"), ("qx", [2, NL, 8], "float32"), ("qp", [2, NL, 2, 8], "float16"),
+        ("o1", [2, NL, 8, 2, 8], "float16"), ("ei", [W], "int32"), ("xx", [W], "int32"), ("n32", [W], "float32"),
+        ("az", [W], "int32"), ("sf", [W], "int32"), ("b2", [W], "int32"), ("n2", [2, W], "int32"), ("sl", [W], "int32"),
+        ("dl", [W], "bfloat16"), ("ii", [W], "bfloat16"), ("nb", [W], "bfloat16"), ("ni", [W], "int32"),
+        ("q2", [2, NL, 32], "float16"), ("o2", [2, NL, 16, 17], "float16"), ("fi", [W], "int32"),
+        ("nm1", [NL, 16], "int32"), ("nm2", [NL, 16], "int32"), ("nm3", [NL, 16], "int32"),
+        ("tm", [NL, 2, 16], "float32"), ("tt", [NL, 2, 16], "float32"), ("l0", [W], "uint16"),
+        ("ml1", [W], "uint16"), ("ml2", [W], "uint16"), ("le2", [W], "uint16"), ("le3", [W], "uint16"), ("ls3", [W], "uint16"),
+        ("len2", [NL, 16], "int32"), ("len3", [NL, 16], "int32"), ("lsn3", [NL, 16], "int32"),
+        ("yo2", [W], "float32"), ("yo3", [W], "float32"), ("ly2", [W], "float32"), ("ly3", [W], "float32")):
+    SCRATCH[_n] = ("sbuf", [128, H] + _s, _d)
+SEMAPHORES = ["ldc", "lde", "lds", "out", "loc", "vec", "act", "pe", "gp", "ls2", "lsn2"] + [
+    "%s%d" % (_a, _h) for _a in ("le2", "le3", "ls3", "len2", "len3", "lsn3", "ly2", "ly3") for _h in range(H)]
+
+
+def rank_program(g, core, T, topo):
+    rank = T.rank_of(core)
+    if rank is None:
+        return
+    N = len(T.cores)
+    nxt = T.cores[(rank + 3) % N]
+    prv = T.cores[(rank + 7) % N]
+    opp = T.cores[(rank + 4) % N]
+    queue = {"v": g.vector, "s": g.scalar, "p": g.tensor, "g": g, "y": g.sync}
+    engsem = {"v": "vec", "s": "act", "p": "pe", "g": "gp"}
+    ops, lastw, rds, banks = [], {}, {}, {}
+
+    def op(eng, cost, fn, r=(), w=(), bank=(), sem=None, val=0, lat=0.0):
+        i = len(ops)
+        dep = set()
+        for k in r:
+            if k in lastw: dep.add(lastw[k])
+        for k in w:
+            if k in lastw: dep.add(lastw[k])
+            dep.update(rds.get(k, ()))
+        for b in bank:
+            dep.update(j for e, j in banks.setdefault(b, {}).items() if e != eng)
+            banks[b][eng] = i
+        dep.discard(i)
+        for k in r: rds.setdefault(k, []).append(i)
+        for k in w: lastw[k] = i; rds[k] = []
+        ops.append(dict(eng=eng, cost=cost, fn=fn, dep=dep, sem=sem, val=val, lat=lat))
+        return i
+
+    def V(n, fn, r=(), w=(), bank=()):
+        op("v", VO + n * CY, fn, r, w, bank)
+
+    def S(n, fn, r=(), w=(), bank=()):
+        op("s", SO + n * CY, fn, r, w, bank)
+
+    def P(n, fn, r=(), w=(), bank=()):
+        op("p", n * PCY, fn, r, w, bank)
+
+    v, s, te = g.vector, g.scalar, g.tensor
+    B = lambda n, h: T[n][:, h]
+    ts, tt, scan, act, mm = v.tensor_scalar, v.tensor_tensor, v.tensor_tensor_scan, s.activation, te.matmul
+
+    def dma(eng, q, out, in_, sem, w, lat):
+        op(eng, 60.0, lambda: [(q.dma_start(out, in_), sem, 16)], (), w, sem=sem, val=16, lat=lat)
+
+    dma("y", g.sync, T.en[:], T.enz[:], "lde", ["en"], 2000.0)
+    dma("s", g.scalar, T.su[:], T.subs[:], "lds", ["su"], 2000.0)
+    dma("y", g.sync, T.ct[:], T.cont[:], "ldc", ["ct"], 6000.0)
+
+    V(128, lambda: v.memset(T.one[:], 1.0), w=["one"])
+    op("g", 140, lambda: g.iota(T.pid[:], [[0, 1]], 0, 1), w=["pid"])
+    V(1, lambda: ts(T.pbit[:], T.pid[:], 16, None, A.bitwise_and), ["pid"], ["pbit"])
+    V(1, lambda: ts(T.modd[:], T.pbit[:], 1.0 / 16, None, A.mult), ["pbit"], ["modd"])
+    V(1, lambda: ts(T.meven[:], T.pbit[:], -1.0 / 16, 1.0, A.mult, A.add), ["pbit"], ["meven"])
+    op("g", 380, lambda: g.affine_select(T.idf[:], T.one[:], [[-1, 128]], A.is_equal, 0.0, 0, 1), ["one"], ["idf"])
+    V(8, lambda: v.memset(T.g8a[:], 1.0), w=["g8a"])
+    op("g", 190, lambda: g.affine_select(T.g8b[:], T.g8a[:], [[-16, 8]], A.is_ge, 0.0, 0, 1), ["g8a"], ["g8b"])
+    op("g", 190, lambda: g.affine_select(T.g8c[:], T.g8b[:], [[16, 8]], A.is_ge, 0.0, 15, -1), ["g8b"], ["g8c"])
+
+    def initial(k, src):
+        xm, xt, nm = T["xm" + k], T["xt" + k], T["nm" + k]
+        V(192, lambda: ts(xm[:, :, 0, :], T[src][:], T.meven[:], None, A.mult), [src, "meven"], ["xm0" + k])
+        V(192, lambda: ts(xm[:, :, 1, :], T[src][:], T.modd[:], None, A.mult), [src, "modd"], ["xm1" + k])
+        V(384, lambda: v.transpose(xt[:, :, :, :], xm[:, :, :, :]), ["xm0" + k, "xm1" + k], ["xt" + k])
+        V(384, lambda: tt(nm[:], xt[:, :, 0, :], xt[:, :, 1, :], A.add), ["xt" + k], ["nm" + k])
+
+    def lists(dst, src3, rk, wk):
+        for c in range(NL):
+            V(16, lambda c=c: v.tensor_copy(dst[:, c:W:NL], src3[:, c, :]), rk, [(wk, c)])
+
+    initial("e", "en")
+    for h in range(H):
+        lists(T.m0l[:, h], T.nme[:, NL * h:NL * h + NL, :], ["nme"], ("m0l", h))
+        if h == 0:
+            initial("s", "su")
+        lists(B("l0", h), T.nms[:, NL * h:NL * h + NL, :], ["nms"], ("l0", h))
+        if h == 0:
+            for n, val, d in IDENT:
+                if d == "float16":
+                    V(128, lambda n=n, val=val: ts(T[n][:], T.idf[:], val, None, A.mult), ["idf"], [n])
+                else:
+                    S(128, lambda n=n, val=val: act(T[n][:], T.idf[:], F.Copy, scale=val), ["idf"], [n])
+            for n, val in (("selc", 0.5), ("seld", 65536.0)):
+                V(80, lambda n=n: v.memset(T[n][:], 0.0), w=[n])
+                V(8, lambda n=n, val=val: ts(T[n][:, 15:143:16], T.g8c[:], val, None, A.mult), ["g8c"], [n])
+            V(W / 2, lambda: v.memset(T.kc8[:], 8.0), w=["kc8"])
+            for n, pat, base in (("krow", [[4096, 16], [0, NL]], 0), ("kkeep", [[0, NL], [256, 16]], -2048), ("kfill", [[0, NL], [256, 16]], 2048)):
+                op("g", 300, lambda n=n, pat=pat, base=base: g.iota(T[n][:], pat, base, 0, allow_small_or_imprecise_dtypes=True), w=[n])
+            for n, val in (("x17", 0.0), ("a17", 0), ("pb", 0)):
+                V(H * W17, lambda n=n, val=val: v.memset(T[n][:], val), w=[(n, q) for q in range(H)])
+            for n in ("mx", "mn"):
+                V(8, lambda n=n: v.memset(T[n][:, :, W17:W17 + 4], 0.0), w=[(n + "pad", q) for q in range(H)])
+            for n, base, at, val, m in (("rk17", 0.0, (0,), BIG, 17), ("mk17", 1.0, (0,), 0.0, 17), ("rm17", 0.0, (15, 16), -1.0e6, 17),
+                                        ("rn17", 0.0, (15, 16), 1.0e6, 17), ("tg17", 4096.0, (0,), -1.0e6, 17), ("kw", 2128.0, (15,), -1968.0, 17),
+                                        ("mk16", 1.0, (0,), 0.0, 16), ("rm16", 0.0, (15,), -1.0e6, 16)):
+                V(W17, lambda n=n, base=base: v.memset(T[n][:], base), w=[n])
+                for a in at:
+                    V(NL, lambda n=n, a=a, val=val, m=m: v.memset(T[n][:, a::m], val), w=[n])
+    nloc = [0]
+
+    def send(dst, land, out, in_, w, r):
+        rid, pid = topo.addr(dst, core)
+        m, ne = topo.mask(core, dst), len(topo.engines(core, dst))
+        nloc[0] += ne
+        i = op("g", 300, lambda: [(g.remote_dma(out, in_, T.sem[land], T.sem.loc, pid, rid, m), None, 0)], r)
+        j = op("r", 0, None, (), w, sem=land, val=ne, lat=RLAT)
+        ops[j]["dep"].add(i)
+
+    send(opp, "ls2", T.ls2[:], T.m0l[:], ["ls2"], [(("m0l", h), c) for h in range(H) for c in range(NL)])
+    send(opp, "lsn2", T.lsn2[:], T.nme[:], ["lsn2"], ["nme"])
+
+    dn = [0]
+    pw = T.pw
+    for t in range(1, R + 1):
+        for h in range(H):
+            b = lambda n: B(n, h)
+            K = lambda *n: [(x, h) for x in n]
+            eb = "pe%d" % ((t * H + h) % 2)
+            pE = T[eb]
+            ck = T.pck[:, h % CKS, :, :, 0:NL]
+            w0, w1 = pw[:, 2 * h, 0:W], pw[:, 2 * h + 1, 0:W]
+            k0, k1 = [("pw", 2 * h)], [("pw", 2 * h + 1)]
+            cs = slice(NL * h, NL * h + NL)
+            if t == 1:
+                el, ek = T.m0l[:, h], [(("m0l", h), c) for c in range(NL)]
+                sl, sk = b("l0"), [(("l0", h), c) for c in range(NL)]
+                en, enk, zn, znk = T.nme[:, cs, :], ["nme"], T.nms[:, cs, :], ["nms"]
+            else:
+                el, ek, en, enk = b("le%d" % t), K("le%d" % t), b("len%d" % t), K("len%d" % t)
+                if t == 2:
+                    sl, sk, zn, znk = T.ls2[:, h], ["ls2"], T.lsn2[:, cs, :], ["lsn2"]
+                else:
+                    sl, sk, zn, znk = b("ls3"), K("ls3"), b("lsn3"), K("lsn3")
+            def gather(n, l, lk, a, z):
+                for c in range(a, z, 64):
+                    e = min(c + 64, z)
+                    S(16 * (e - c) * 1.55, lambda c=c, e=e, y=b(n): act(y[:, 16 * (c - a):16 * (e - a)], T.ct[:].indirect(l[:, c:e]), F.Copy), ["ct"] + lk, [(n, h, c)])
+                return [(n, h, c) for c in range(a, z, 64)]
+            v15k = gather("v15", el, ek, W - NL, W)
+            yk = gather("y", sl, sk, 0, W)
+            for q in range(len(yk)): ops[-1 - q]["late"] = True
+            vk = gather("v", el, ek, 0, W)
+
+            def vdiff(q, p, x):
+                a = PC * q
+                mm(p[:, 0:PC], T.ip[:], x[:, a:a + PC], True, False)
+                if q < NP - 1:
+                    return mm(p[:, 0:PC], T.im[:], x[:, a + W:a + W + PC], False, True)
+                mm(p[:, 0:PC - W], T.im[:], x[:, a + W:NV], False, False)
+                return mm(p[:, PC - W:PC], T.im[:], x[:, 0:W], False, True)
+
+            def ydiff(q, p, y, x):
+                mm(p[:, 0:PC], T.ip[:], y[:, PC * q:PC * q + PC], True, False)
+                for i in range(RP):
+                    z = mm(p[:, W * i:W * i + W], T.im[:], x[:], False, i == RP - 1)
+                return z
+
+            def sums(p, sel, x, con):
+                for m in range(16):
+                    mm(p, sel[:, 15 - m:143 - m], x[:, m:NV:16], m == 0, False)
+                return mm(p, T.ip[:], con[:], False, True)
+
+            for kind in (1, 0):
+                for q in range(NP):
+                    pn = "pd%d" % (dn[0] % NDIFF); dn[0] += 1
+                    a, z = PC * q, PC * q + PC
+                    if kind == 0:
+                        P(2 * PC, lambda q=q, p=T[pn], x=b("v"), f=vdiff: f(q, p, x), vk + ["ip", "im"], [pn], [pn])
+                        S(PC, lambda a=a, z=z, p=T[pn], o=b("sg"): act(o[:, a:z], p[:, 0:PC], F.Sign, bias=-0.5), [pn], [("sg", h, q)], [pn])
+                    else:
+                        P(2 * PC, lambda q=q, p=T[pn], y=b("y"), x=b("v15"), f=ydiff: f(q, p, y, x), v15k + yk + ["ip", "im"], [pn], [pn])
+                        S(PC, lambda a=a, z=z, p=T[pn], o=b("ab"): act(o[:, a:z], p[:, 0:PC], F.Abs), [pn], [("ab", h, q)], [pn])
+            P(17 * W, lambda p=ck[:, 1], x=b("ab"), f=sums: f(p, T.seld, x, T.krow), [("ab", h, q) for q in range(NP)] + ["seld", "ip", "krow"], K("pk"), ["pck"])
+            P(17 * W, lambda p=ck[:, 0], x=b("sg"), f=sums: f(p, T.selc, x, T.kc8), [("sg", h, q) for q in range(NP)] + ["selc", "ip", "kc8"], K("pc"), ["pck"])
+            for c in range(NL):
+                S(32, lambda c=c, p=ck, x=b("x17"): act(x[:, :, 17 * c:17 * c + 16], p[:, :, :, c], F.Copy), K("pc", "pk"), [("x17", h, c)], ["pck"])
+            x17k = [("x17", h)] + [("x17", h, c) for c in range(NL)]
+            V(W, lambda o=b("s2"), x=en: ts(o[:, 0, :, :], x[:], 7, None, A.arith_shift_right), enk, K("s2h"))
+            V(W, lambda o=b("sl"), x=en: ts(o[:], x[:], 127, None, A.bitwise_and), enk, K("sl"))
+            V(2 * W, lambda o=b("s2"), x=b("sl"): tt(o[:, 1, :, :], x[:], o[:, 0, :, :], A.add), K("sl", "s2h"), K("s2l"))
+            V(W17, lambda x=b("x17"), o=b("cc"): scan(o[:], T.mk17[:], x[:, 0, :], 0.0, A.mult, A.add), x17k + ["mk17"], K("cc"))
+            V(W17, lambda x=b("x17"), o=b("km"): scan(o[:], T.rk17[:], x[:, 1, :], 0.0, A.add, A.min), x17k + ["rk17"], K("km"))
+            V(W17, lambda x=b("cc"), o=b("par"): ts(o[:], x[:], 1, None, A.bitwise_and), K("cc"), K("par"))
+            V(NL, lambda x=b("km"), o=b("pb"): ts(o[:, 0::17], x[:, 15::17], 4096, None, A.bitwise_and), K("km"), K("pb"))
+            V(W17, lambda x=b("par"), o=b("st"): ts(o[:], x[:], -8192.0, 4096.0, A.mult, A.add), K("par"), K("st"))
+            V(W17, lambda x=b("pb"), o=b("od"): scan(o[:], T.tg17[:], x[:], 0.0, A.subtract, A.max), K("pb") + ["tg17"], K("od"))
+            V(NL, lambda x=b("km"), o=b("st"): ts(o[:, 0::17], x[:, 15::17], 61440, None, A.bitwise_and), K("km"), K("st"))
+            V(W17, lambda x=b("st"), o=b("pos"): scan(o[:], T.mk17[:], x[:], 0.0, A.mult, A.add), K("st") + ["mk17"], K("pos"))
+            V(W17, lambda x=b("pos"), o=b("mx"): scan(o[:, W17 - 1::-1], T.rm17[:, ::-1], x[:, ::-1], 0.0, A.add, A.max), K("pos") + ["rm17"], K("mx"))
+            V(W17, lambda x=b("pos"), o=b("mn"): scan(o[:, W17 - 1::-1], T.rn17[:, ::-1], x[:, ::-1], 0.0, A.add, A.min), K("pos") + ["rn17"], K("mn"))
+            S(W17, lambda x=b("pos"), o=b("g1"): act(o[:], x[:], F.Sign, bias=63488.0, scale=-1.0), K("pos"), K("g1"))
+            S(W17, lambda x=b("pos"), o=b("g2"): act(o[:], x[:], F.Sign, bias=-2048.0, scale=-1.0), K("pos"), K("g2"))
+            S(W17, lambda x=b("x17"), o=b("w"): act(o[:], x[:, 0, :], F.Sign, bias=-9.5), x17k, K("w"))
+            if t > 1:
+                V(2 * W17, lambda x=b("x17"), o=b("d1"), a=b("a17"): tt(o[:], x[:, 0, :], a[:], A.subtract), x17k + K("a17"), K("d1"))
+            dk, dx = (K("d1"), b("d1")) if t > 1 else (x17k, b("x17")[:, 0, :])
+            S(W17, lambda x=dx, o=b("u"): act(o[:], x[:], F.Sign, bias=5.5, scale=-1.0), dk, K("u"))
+
+            def usum(p, h):
+                o = p[:, 0:NL, 32:49]
+                mm(o, T.ip[:], T.kw[:], True, False)
+                for n, c in (("od", "i4"), ("w", "i16"), ("u", "i32"), ("pos", "i16th"), ("g1", "i2048"), ("g2", "i2048")):
+                    mm(o, T[c][:], B(n, h)[:], False, False)
+                mm(o, T.im[:], B("mx", h)[:, 0:W17], False, False)
+                mm(o, T.ip[:], B("mx", h)[:, 1:W17 + 1], False, False)
+                mm(o, T.ip[:], B("mn", h)[:, 0:W17], False, False)
+                return mm(o, T.im[:], B("mn", h)[:, 1:W17 + 1], False, True)
+            P(11 * W17, lambda p=pE, h=h: usum(p, h), K("od", "pos", "g1", "g2", "u", "w", "mx", "mn", "mxpad", "mnpad") + ["ip", "im", "i16th", "i16", "i4", "i32", "i2048", "kw"], ["U" + eb], [eb])
+            for a, sk2 in ((0, "s2h"), (1, "s2l")):
+                V(W, lambda a=a, o=b("q1"), x=b("s2"), p=pE: tt(o[:, a, :, :], x[:, a, :, :], p[:, 0:NL, 32:48], A.add), K(sk2) + ["U" + eb], K("q1%d" % a), [eb])
+            V(2 * W, lambda o=b("qx"), x=b("q1"): tt(o[:], x[:, :, :, 0::2], x[:, :, :, 1::2], A.max), K("q10", "q11"), K("qx"))
+            V(2 * W, lambda o=b("qp"), x=b("q1"): tt(o[:, :, :, 0, :], x[:, :, :, 0::2], x[:, :, :, 1::2], A.min), K("q10", "q11"), K("qpe"))
+            V(W, lambda o=b("qp"), x=b("qx"): ts(o[:, :, :, 1, :], x[:], -16640.0, None, A.add), K("qx"), K("qpo"))
+            for p_ in range(8):
+                V(W, lambda p_=p_, o=b("o1"), x=b("qp"): ts(o[:, :, :, p_, :, :], x[:], 512.0 * p_ - 2048.0, 512.0 * p_ - 1792.0, A.max, A.min), K("qpe", "qpo"), [("o1", h, p_)])
+
+            def picked(p, q, o, n, f):
+                for k in range(n):
+                    for a, c in ((0, T.i127h), (1, T.iph)):
+                        x = o[:, a, :, 8 * f:8 * f + 8, k] if n == 17 else o[:, a, :, 4 * f:4 * f + 4, :, k]
+                        z = mm(p[:, 0:NL, q + 8 * f:q + 8 * f + 8], c[:], x, k == 0 and a == 0, k == n - 1 and a == 1)
+                return z
+            for f in range(2):
+                P(16 * max(64, W // 2), lambda p=pE, o=b("o1"), f=f, pk=picked: pk(p, 0, o, 8, f), [("o1", h, p_) for p_ in range(4 * f, 4 * f + 4)] + ["iph", "i127h"], ["E%d" % f + eb], [eb])
+            V(W, lambda o=b("ei"), p=pE: v.tensor_copy(o[:], p[:, 0:NL, 0:16]), ["E0" + eb, "E1" + eb], K("ei"), [eb])
+            V(W, lambda o=b("xx"), x=b("ei"): ts(o[:], x[:], 16383, None, A.bitwise_and), K("ei"), K("xx"))
+            V(W, lambda x=b("xx"), o=b("dl"): ts(o[:], x[:], 12288.0, None, A.is_ge), K("xx"), K("dl"))
+            V(W, lambda x=b("dl"), o=b("ii"): scan(o[:], T.mk16[:], x[:], 0.0, A.mult, A.add), K("dl") + ["mk16"], K("ii"))
+            V(W, lambda x=b("ii"), o=b("nb"): scan(o[:, ::-1], T.rm16[:, ::-1], x[:, ::-1], 0.0, A.add, A.max), K("ii") + ["rm16"], K("nb"))
+
+            def tsum(p, h):
+                o = p[:, 0:NL, 32:48]
+                mm(o, T.ip[:], T.kkeep[:], True, False)
+                mm(o, T.i8192[:], B("dl", h)[:], False, False)
+                mm(o, T.im256[:], B("ii", h)[:], False, True)
+                o = p[:, 0:NL, 0:16]
+                mm(o, T.ip[:], T.kfill[:], True, False)
+                return mm(o, T.im256[:], B("nb", h)[:], False, True)
+            P(5 * W, lambda p=pE, h=h: tsum(p, h), K("dl", "ii", "nb") + ["i8192", "im256", "ip", "kkeep", "kfill"], ["T" + eb, "U" + eb, "E0" + eb, "E1" + eb], [eb])
+            V(W, lambda x=b("xx"), o=w0: ts(o, x[:], -8192.0, 0.0, A.add, A.max), K("xx"), k0)
+            V(W, lambda x=b("xx"), o=b("n32"): ts(o[:], x[:], 4096.0, 32.0, A.is_lt, A.mult), K("xx"), K("n32"))
+            V(W, lambda x=b("xx"), o=w1, t=t: ts(o, x[:], 8192.0, 77.0 * t, A.is_ge, A.mult), K("xx"), k1)
+            V(W, lambda x=b("n32"), o=w0: tt(o, x[:], o, A.add), K("n32"), k0)
+            V(W, lambda x=b("xx"), o=w1: tt(o, x[:], o, A.add), K("xx"), k1)
+            V(W, lambda x=zn, o=b("az"), y=w0: tt(o[:], x, y, A.mult), znk + k0, K("az"))
+            V(W, lambda x=b("az"), o=b("sf"): ts(o[:], x[:], 5, 4095, A.arith_shift_right, A.bitwise_and), K("az"), K("sf"))
+            V(W, lambda x=b("sf"), o=b("b2"), y=w1: tt(o[:], x[:], y, A.add), K("sf") + k1, K("b2"))
+            V(W, lambda x=b("b2"), o=b("n2"): ts(o[:, 0, :], x[:], 7, 31, A.arith_shift_right, A.bitwise_and), K("b2"), K("n2h"))
+            V(W, lambda x=b("b2"), o=b("n2"): ts(o[:, 1, :], x[:], 127, None, A.bitwise_and), K("b2"), K("n2l"))
+            for a, sk2 in ((0, "s2h"), (1, "s2l")):
+                V(W, lambda a=a, o=b("q2"), x=b("s2"), p=pE: tt(o[:, a, :, 16:32], x[:, a, :, :], p[:, 0:NL, 0:16], A.add), K(sk2) + ["T" + eb], K("q2b%d" % a), [eb])
+            V(W, lambda x=b("n2"), p=pE, o=w0: tt(o, x[:, 0, :], p[:, 0:NL, 32:48], A.add), K("n2h") + ["T" + eb], k0, [eb])
+            V(W, lambda x=b("n2"), o=b("q2"), y=w0: tt(o[:, 1, :, 0:16], x[:, 1, :], y, A.add), K("n2l") + k0, K("q2a1"))
+            V(W, lambda o=b("q2"), y=w0: v.tensor_copy(o[:, 0, :, 0:16], y), k0, K("q2a0"))
+            for i in range(16):
+                V(W17, lambda i=i, o=b("o2"), x=b("q2"): ts(o[:, :, :, i, :], x[:, :, :, i:i + 17], 256.0 * i - 2048.0, 256.0 * i - 1792.0, A.max, A.min), K("q2a0", "q2a1", "q2b0", "q2b1"), [("o2", h, i)])
+            for f in range(2):
+                P(34 * max(64, W // 2), lambda p=pE, o=b("o2"), f=f, pk=picked: pk(p, 16, o, 17, f), [("o2", h, i) for i in range(8 * f, 8 * f + 8)] + ["iph", "i127h"], ["R%d" % f + eb], [eb])
+            nm, nmk = b("nm%d" % t), K("nm%d" % t)
+            V(W, lambda o=b("fi"), p=pE: v.tensor_copy(o[:], p[:, 0:NL, 16:32]), ["R0" + eb, "R1" + eb], K("fi"), [eb])
+            V(W, lambda o=nm, x=b("fi"): ts(o[:], x[:], 4095, None, A.bitwise_and), K("fi"), nmk)
+            if t < R:
+                n = t + 1
+                lists(b("ml%d" % t), nm, nmk, ("ml%d" % t, h))
+                mk = [(("ml%d" % t, h), c) for c in range(NL)]
+                send(nxt, "le%d%d" % (n, h), b("le%d" % n)[:], b("ml%d" % t)[:], K("le%d" % n), mk)
+                send(nxt, "len%d%d" % (n, h), b("len%d" % n)[:], nm[:], K("len%d" % n), nmk)
+                if t + 2 <= R:
+                    send(prv, "ls3%d" % h, b("ls3")[:], b("ml%d" % t)[:], K("ls3"), mk)
+                    send(prv, "lsn3%d" % h, b("lsn3")[:], nm[:], K("lsn3"), nmk)
+                V(W, lambda x=b("nb"), o=b("ni"): v.tensor_copy(o[:], x[:]), K("nb"), K("ni"))
+                V(W, lambda x=b("ni"), o=b("a17"): ts(o[:, :, 0:16], x[:], 1, None, A.bitwise_and), K("ni"), K("a17"))
+            if t >= R - 1:
+                V(W, lambda x=nm, o=b("tm"): ts(o[:, :, 0, :], x[:], T.meven[:], None, A.mult), nmk + ["meven"], K("tm0"))
+                V(W, lambda x=nm, o=b("tm"): ts(o[:, :, 1, :], x[:], T.modd[:], None, A.mult), nmk + ["modd"], K("tm1"))
+                V(2 * W, lambda x=b("tm"), o=b("tt"): v.transpose(o[:], x[:]), K("tm0", "tm1"), K("tt"))
+                V(2 * W, lambda x=b("tt"), o=b("yo%d" % t): tt(o[:], x[:, :, 0, :], x[:, :, 1, :], A.add), K("tt"), K("yo%d" % t))
+                send(nxt if t == R else prv, "ly%d%d" % (t, h), b("ly%d" % t)[:], b("yo%d" % t)[:], K("ly%d" % t), K("yo%d" % t))
+                y = T.yenz if t == R else T.ysub
+                op("y", 60, lambda y=y, x=b("ly%d" % t), h=h: [(g.sync.dma_start(y[:, W * h:W * h + W], x[:]), "out", 16)], K("ly%d" % t))
+
+    n = len(ops)
+    succ = [[] for i in range(n)]
+    for i, o in enumerate(ops):
+        for d in o["dep"]: succ[d].append(i)
+        o["pr"] = i + (LATE if o.get("late") else 0)
+    by_pr = sorted(range(n), key=lambda i: ops[i]["pr"])
+
+    def schedule(known):
+        left = [len(o["dep"]) for o in ops]
+        ready = [0.0] * n
+        free, order, cand, urgent, out = {}, [], {}, {}, set()
+        if known:
+            for i in by_pr: urgent.setdefault(ops[i]["eng"], []).append(i)
+        end = 0.0
+        for i in range(n):
+            if not left[i]: cand.setdefault(ops[i]["eng"], []).append(i)
+        while True:
+            best = None
+            for e, c in cand.items():
+                if not c: continue
+                f = free.get(e, 0.0) if e != "r" else 0.0
+                starts = []
+                for i in c:
+                    st = max(ready[i], f)
+                    if known and ops[i]["cost"] > HOLD:
+                        lim = st + AHEAD * ops[i]["cost"]
+                        for j in urgent[e]:
+                            if ops[j]["pr"] >= ops[i]["pr"]: break
+                            if j not in out and left[j] and st < known[j] < lim: st = known[j] + 1.0
+                    starts.append((st, i))
+                lo = min(starts)[0]
+                pr, st, i = min((ops[i]["pr"], st, i) for st, i in starts if st <= lo + 20.0)
+                if best is None or (st, i) < best[0]: best = ((st, i), e, i)
+            if best is None: break
+            (st, _), e, i = best
+            cand[e].remove(i)
+            out.add(i)
+            free[e] = st + ops[i]["cost"]
+            fin = free[e] + ops[i]["lat"]
+            end = max(end, fin)
+            order.append(i)
+            for j in succ[i]:
+                ready[j] = max(ready[j], fin + WAKE)
+                left[j] -= 1
+                if not left[j]: cand.setdefault(ops[j]["eng"], []).append(j)
+        return end, order, ready
+
+    best, known = None, None
+    for k in range(PASSES):
+        end, order, known = schedule(known)
+        if best is None or end < best[0]: best = (end, order)
+
+    count, done, waited, ndma = {}, {}, {}, 0
+    for i in best[1]:
+        o = ops[i]
+        e = o["eng"]
+        if e == "r":
+            done[i] = (o["sem"], o["val"])
+            continue
+        need = {}
+        for d in o["dep"]:
+            sm, val = done[d]
+            need[sm] = max(need.get(sm, 0), val)
+        for sm in sorted(need):
+            if waited.get((e, sm), 0) < need[sm]:
+                queue[e].wait_ge(T.sem[sm], need[sm])
+                waited[(e, sm)] = need[sm]
+        x = o["fn"]()
+        if isinstance(x, list):
+            ins, sm, inc = x[0]
+            if sm is not None:
+                ins.then_inc(T.sem[sm], inc)
+                if sm == "out": ndma += inc
+            done[i] = (sm, o["val"]) if sm else ("loc", 0)
+        else:
+            sm = engsem[e]
+            x.then_inc(T.sem[sm], 1)
+            count[sm] = count.get(sm, 0) + 1
+            done[i] = (sm, count[sm])
+    g.sync.wait_ge(T.sem.out, ndma)
+    g.wait_ge(T.sem.loc, nloc[0])
+    for sm in count:
+        g.wait_ge(T.sem[sm], count[sm])

@@ -1,68 +1,73 @@
-from concourse.bass import DstId, RemoteDMATransfer
-from concourse.mybir import dt, AluOpType as A, ActivationFunctionType as F
+from concourse.mybir import AluOpType as A, ActivationFunctionType as F
 
 H = 2
 NL = 12 // H
-W, W17 = 16 * NL, 17 * NL
-NV = 16 * W
-RP = 8 if NL <= 4 else 4
-NP, PC = 16 // RP, RP * W
+W = 16 * NL
 R = 3
-CY, VO, SO, PCY = 0.83, 50.0, 65.0, 0.42
-LATE, HOLD, AHEAD, PASSES, WAKE, RLAT = 100, 400.0, 0.8, 4, 60.0, 2500.0
+RB = 4 if NL > 4 else 8
+ESPLIT, RSPLIT = (0, 2, 4, 6, 7, 8), (0, 2, 4, 6, 8, 10, 12, 14, 16, 17)
+ON = dict(H="v", F="v", hn="s", h="v", nm="s", B="v", lo="s")
+TWICE = False
+SIGNV = False
+GV = {(1, 0, "y"): 6, (1, 1, "y"): 6}
+CY, VO, SO, PCY, GA = 0.83, 40.0, 55.0, 0.48, 1.55
+WAKE, RLAT, PASSES, STAG = 60.0, 2700.0, 8, 6000.0
 BIG = 1.0e9
-CKS = 4 if NL <= 4 else 2
 NDIFF = 4
+KEY = 512.0
 
-IDENT = (("ip", 1.0, "bfloat16"), ("im", -1.0, "bfloat16"), ("i16th", 1.0 / 16, "bfloat16"), ("i2048", 2048.0, "bfloat16"),
-         ("i16", 16.0, "bfloat16"), ("i32", 32.0, "bfloat16"), ("i4", 4.0, "bfloat16"), ("i8192", 8192.0, "bfloat16"),
-         ("im256", -256.0, "bfloat16"), ("iph", 1.0, "float16"), ("i127h", 127.0, "float16"))
+IDENT = (("ip", 1.0, "bfloat16"), ("im", -1.0, "bfloat16"), ("iH", -31 * KEY, "bfloat16"), ("im8", -8 * KEY, "bfloat16"),
+         ("ip8", 8 * KEY, "bfloat16"), ("ip16", 16 * KEY, "bfloat16"), ("iw", 32.0, "bfloat16"), ("iu", 96.0, "bfloat16"),
+         ("im63", -63.0, "bfloat16"), ("it1", 38.5, "bfloat16"), ("it2", 77.0, "bfloat16"), ("it3", 115.5, "bfloat16"),
+         ("i64", 64.0, "bfloat16"), ("im64", -64.0, "bfloat16"),
+         ("iR", -65 * 64.0, "bfloat16"), ("ia", -1.0 / 128, "bfloat16"), ("ib", 1.0 / 64, "bfloat16"),
+         ("iph", 1.0, "float16"), ("i64h", 64.0, "float16"), ("iKh", KEY, "float16"), ("i63h", 63.0, "float16"))
+C0 = 0.0 if SIGNV else 8.0
+FILLS = (("k1", 1.0, None, 0, "bfloat16"), ("kres", 136.0, None, 0, "bfloat16"), ("k28", 28.0, None, 0, "float16"),
+         ("kc1", C0, None, 0, "float16"), ("kc2", C0 + 1.0 / 128 - 272.0 / 128, None, 0, "float16"),
+         ("mk", 1.0, 0, 0.0, "bfloat16"), ("rk", 0.0, 0, BIG, "float32"),
+         ("rz", 0.0, 15, -1024.0, "bfloat16"), ("rm", 0.0, 15, -1024.0, "bfloat16"), ("rn", 0.0, 15, 1024.0, "bfloat16"))
 SCRATCH = {
     "ct": ("sbuf", [128, 4096], "bfloat16"),
     "en": ("sbuf", [128, 192], "int32"), "su": ("sbuf", [128, 192], "int32"),
     "one": ("sbuf", [128, 128], "float32"), "idf": ("sbuf", [128, 128], "float32"),
+    "iup": ("sbuf", [128, 128], "float32"), "idn": ("sbuf", [128, 128], "float32"),
     "g8a": ("sbuf", [128, 8], "float32"), "g8b": ("sbuf", [128, 8], "float32"), "g8c": ("sbuf", [128, 8], "float32"),
     "pid": ("sbuf", [128, 1], "int32"), "pbit": ("sbuf", [128, 1], "int32"),
     "modd": ("sbuf", [128, 1], "float32"), "meven": ("sbuf", [128, 1], "float32"),
     "selc": ("sbuf", [128, 160], "bfloat16"), "seld": ("sbuf", [128, 160], "bfloat16"),
-    "kc8": ("sbuf", [128, W], "bfloat16"), "krow": ("sbuf", [128, W], "bfloat16"),
-    "kw": ("sbuf", [128, W17], "bfloat16"), "tg17": ("sbuf", [128, W17], "float32"),
-    "kkeep": ("sbuf", [128, W], "bfloat16"), "kfill": ("sbuf", [128, W], "bfloat16"),
-    "mk17": ("sbuf", [128, W17], "float32"), "rk17": ("sbuf", [128, W17], "float32"),
-    "rm17": ("sbuf", [128, W17], "float32"), "rn17": ("sbuf", [128, W17], "float32"),
-    "mk16": ("sbuf", [128, W], "float32"), "rm16": ("sbuf", [128, W], "float32"),
-    "m0l": ("sbuf", [128, H, W], "uint16"), "ls2": ("sbuf", [128, H, W], "uint16"), "lsn2": ("sbuf", [128, 12, 16], "int32"),
-    "nme": ("sbuf", [128, 12, 16], "int32"), "nms": ("sbuf", [128, 12, 16], "int32"),
-    "pck": ("psum", [128, CKS, 2, 16, 16 // CKS], "float32"),
-    "pe0": ("psum", [128, 8, 64], "float32"), "pe1": ("psum", [128, 8, 64], "float32"),
-    "pw": ("psum", [128, 2 * CKS, 256 // CKS], "float32"),
+    "krow": ("sbuf", [128, W], "bfloat16"), "k2k": ("sbuf", [128, 192], "float16"),
+    "ku": ("sbuf", [128, 2, W], "float16"), "kt": ("sbuf", [128, 4, W], "bfloat16"),
+    "swp": ("sbuf", [128, 2, 2, 128], "float16"),
+    "xf": ("sbuf", [128, 2, 192], "float16"), "xt": ("sbuf", [128, 2, 12, 16], "float16"),
+    "le1": ("sbuf", [128, 192], "uint16"), "ls1": ("sbuf", [128, 192], "uint16"), "ls2": ("sbuf", [128, 192], "uint16"),
+    "ne1": ("sbuf", [128, 192], "float32"), "ns1": ("sbuf", [128, 192], "float32"), "ns2": ("sbuf", [128, 192], "float32"),
 }
-for _q in range(NDIFF):
-    SCRATCH["pd%d" % _q] = ("psum", [128, 512], "float32")
+for _n in ["pa0", "pa1", "pe0", "pe1"] + ["pd%d" % _q for _q in range(NDIFF)]:
+    SCRATCH[_n] = ("psum", [128, 32, 16] if _n[1] == "d" else [128, 512], "float32")
 for _n, _v, _d in IDENT:
     SCRATCH[_n] = ("sbuf", [128, 128], _d)
-for _k in ("e", "s"):
-    SCRATCH["xm" + _k] = ("sbuf", [128, 12, 2, 16], "float32")
-    SCRATCH["xt" + _k] = ("sbuf", [128, 12, 2, 16], "float32")
+for _n, _a, _b, _c, _d in FILLS:
+    SCRATCH[_n] = ("sbuf", [128, W], _d)
 for _n, _s, _d in (
-        ("v", [NV], "bfloat16"), ("y", [NV], "bfloat16"), ("sg", [NV], "bfloat16"), ("ab", [NV], "bfloat16"), ("v15", [W], "bfloat16"),
-        ("x17", [2, W17], "float32"), ("km", [W17], "int32"), ("cc", [W17], "int32"), ("par", [W17], "int32"),
-        ("st", [W17], "int32"), ("pb", [W17], "int32"), ("od", [W17], "bfloat16"), ("pos", [W17], "bfloat16"),
-        ("g1", [W17], "bfloat16"), ("g2", [W17], "bfloat16"), ("mx", [W17 + 4], "bfloat16"), ("mn", [W17 + 4], "bfloat16"),
-        ("a17", [NL, 17], "int32"), ("d1", [W17], "float32"), ("u", [W17], "bfloat16"), ("w", [W17], "bfloat16"),
-        ("s2", [2, NL, 16], "int32"), ("q1", [2, NL, 16], "float32"), ("qx", [2, NL, 8], "float32"), ("qp", [2, NL, 2, 8], "float16"),
-        ("o1", [2, NL, 8, 2, 8], "float16"), ("ei", [W], "int32"), ("xx", [W], "int32"), ("n32", [W], "float32"),
-        ("az", [W], "int32"), ("sf", [W], "int32"), ("b2", [W], "int32"), ("n2", [2, W], "int32"), ("sl", [W], "int32"),
-        ("dl", [W], "bfloat16"), ("ii", [W], "bfloat16"), ("nb", [W], "bfloat16"), ("ni", [W], "int32"),
-        ("q2", [2, NL, 32], "float16"), ("o2", [2, NL, 16, 17], "float16"), ("fi", [W], "int32"),
-        ("nm1", [NL, 16], "int32"), ("nm2", [NL, 16], "int32"), ("nm3", [NL, 16], "int32"),
-        ("tm", [NL, 2, 16], "float32"), ("tt", [NL, 2, 16], "float32"), ("l0", [W], "uint16"),
+        ("v", [NL, 256], "bfloat16"), ("y", [NL, 256], "bfloat16"), ("sg", [NL, 16, 16], "bfloat16"), ("ab", [NL, 16, 16], "bfloat16"),
+        ("km", [W], "int32"), ("cc", [W], "int32"), ("par", [W], "int32"), ("st", [W], "int32"), ("pos", [W], "bfloat16"),
+        ("mx", [W + 16], "bfloat16"), ("mn", [W + 16], "bfloat16"), ("hp", [W], "bfloat16"), ("fp", [W], "bfloat16"),
+        ("u", [W], "bfloat16"), ("w", [W], "bfloat16"), ("hs", [W], "bfloat16"), ("hn", [W], "bfloat16"),
+        ("sh", [W], "float16"), ("lo", [W], "float32"),
+        ("qb", [2, W // 2], "float32"), ("qx", [W], "float32"), ("qp", [2, NL, 16, 2], "float16"), ("o1", [8, 2, W], "float16"),
+        ("ei", [W], "int32"), ("xx", [W], "int32"), ("n32", [W], "bfloat16"),
+        ("az", [W], "int32"), ("sf", [W], "int32"), ("b2", [W], "int32"), ("n2", [2, W], "int32"),
+        ("dl", [W], "bfloat16"), ("ii", [W], "bfloat16"), ("nb", [W], "bfloat16"),
+        ("q2", [2, NL, 32], "float16"), ("o2", [17, 2, W], "float16"),
+        ("nm", [W], "float32"), ("nh", [NL, 16], "float16"),
         ("ml1", [W], "uint16"), ("ml2", [W], "uint16"), ("le2", [W], "uint16"), ("le3", [W], "uint16"), ("ls3", [W], "uint16"),
-        ("len2", [NL, 16], "int32"), ("len3", [NL, 16], "int32"), ("lsn3", [NL, 16], "int32"),
+        ("ns3", [W], "float32"),
         ("yo2", [W], "float32"), ("yo3", [W], "float32"), ("ly2", [W], "float32"), ("ly3", [W], "float32")):
     SCRATCH[_n] = ("sbuf", [128, H] + _s, _d)
-SEMAPHORES = ["ldc", "lde", "lds", "out", "loc", "vec", "act", "pe", "gp", "ls2", "lsn2"] + [
-    "%s%d" % (_a, _h) for _a in ("le2", "le3", "ls3", "len2", "len3", "lsn3", "ly2", "ly3") for _h in range(H)]
+SEMAPHORES = ["ldc", "lde", "lds", "out", "loc", "vec", "act", "pe", "gp", "ls2", "ns2"] + [
+    "%s%d" % (_a, _h) for _a in ("le2", "le3", "ls3", "ns3", "ly2", "ly3") for _h in range(H)]
+ORDER = []
 
 
 def rank_program(g, core, T, topo):
@@ -75,7 +80,7 @@ def rank_program(g, core, T, topo):
     opp = T.cores[(rank + 4) % N]
     queue = {"v": g.vector, "s": g.scalar, "p": g.tensor, "g": g, "y": g.sync}
     engsem = {"v": "vec", "s": "act", "p": "pe", "g": "gp"}
-    ops, lastw, rds, banks = [], {}, {}, {}
+    ops, lastw, rds, banks, grp = [], {}, {}, {}, [0]
 
     def op(eng, cost, fn, r=(), w=(), bank=(), sem=None, val=0, lat=0.0):
         i = len(ops)
@@ -86,12 +91,13 @@ def rank_program(g, core, T, topo):
             if k in lastw: dep.add(lastw[k])
             dep.update(rds.get(k, ()))
         for b in bank:
-            dep.update(j for e, j in banks.setdefault(b, {}).items() if e != eng)
-            banks[b][eng] = i
+            for e, js in banks.setdefault(b, {}).items():
+                if e != eng: dep.update(js)
+            banks[b][eng] = banks[b].get(eng, [])[-20:] + [i]
         dep.discard(i)
         for k in r: rds.setdefault(k, []).append(i)
         for k in w: lastw[k] = i; rds[k] = []
-        ops.append(dict(eng=eng, cost=cost, fn=fn, dep=dep, sem=sem, val=val, lat=lat))
+        ops.append(dict(eng=eng, cost=cost, fn=fn, dep=dep, sem=sem, val=val, lat=lat, grp=grp[0]))
         return i
 
     def V(n, fn, r=(), w=(), bank=()):
@@ -100,306 +106,290 @@ def rank_program(g, core, T, topo):
     def S(n, fn, r=(), w=(), bank=()):
         op("s", SO + n * CY, fn, r, w, bank)
 
-    def P(n, fn, r=(), w=(), bank=()):
-        op("p", n * PCY, fn, r, w, bank)
+    def P(terms, r=(), w=(), bank=(), start=True, stop=True):
+        def fn():
+            for i, (o, l, x, n) in enumerate(terms):
+                z = g.tensor.matmul(o, l, x, start and i == 0, stop and i == len(terms) - 1)
+            return z
+        ops[op("p", sum(n for o, l, x, n in terms) * PCY, fn, r, w, bank)]["adds"] = not start
 
-    v, s, te = g.vector, g.scalar, g.tensor
-    B = lambda n, h: T[n][:, h]
-    ts, tt, scan, act, mm = v.tensor_scalar, v.tensor_tensor, v.tensor_tensor_scan, s.activation, te.matmul
+    v, s = g.vector, g.scalar
+    ts, tt, scan, act = v.tensor_scalar, v.tensor_tensor, v.tensor_tensor_scan, s.activation
+
+    def affine(name, n, half, out, x, scale, bias, r, w, bank=()):
+        if ON[name] == "v":
+            V(n / 2 if half else n, lambda: ts(out, x, scale, bias, A.mult, A.add), r, w, bank)
+        else:
+            S(n, lambda: act(out, x, F.Identity, bias=bias, scale=scale), r, w, bank)
 
     def dma(eng, q, out, in_, sem, w, lat):
         op(eng, 60.0, lambda: [(q.dma_start(out, in_), sem, 16)], (), w, sem=sem, val=16, lat=lat)
 
-    dma("y", g.sync, T.en[:], T.enz[:], "lde", ["en"], 2000.0)
-    dma("s", g.scalar, T.su[:], T.subs[:], "lds", ["su"], 2000.0)
-    dma("y", g.sync, T.ct[:], T.cont[:], "ldc", ["ct"], 6000.0)
-
-    V(128, lambda: v.memset(T.one[:], 1.0), w=["one"])
-    op("g", 140, lambda: g.iota(T.pid[:], [[0, 1]], 0, 1), w=["pid"])
-    V(1, lambda: ts(T.pbit[:], T.pid[:], 16, None, A.bitwise_and), ["pid"], ["pbit"])
-    V(1, lambda: ts(T.modd[:], T.pbit[:], 1.0 / 16, None, A.mult), ["pbit"], ["modd"])
-    V(1, lambda: ts(T.meven[:], T.pbit[:], -1.0 / 16, 1.0, A.mult, A.add), ["pbit"], ["meven"])
-    op("g", 380, lambda: g.affine_select(T.idf[:], T.one[:], [[-1, 128]], A.is_equal, 0.0, 0, 1), ["one"], ["idf"])
-    V(8, lambda: v.memset(T.g8a[:], 1.0), w=["g8a"])
-    op("g", 190, lambda: g.affine_select(T.g8b[:], T.g8a[:], [[-16, 8]], A.is_ge, 0.0, 0, 1), ["g8a"], ["g8b"])
-    op("g", 190, lambda: g.affine_select(T.g8c[:], T.g8b[:], [[16, 8]], A.is_ge, 0.0, 15, -1), ["g8b"], ["g8c"])
-
-    def initial(k, src):
-        xm, xt, nm = T["xm" + k], T["xt" + k], T["nm" + k]
-        V(192, lambda: ts(xm[:, :, 0, :], T[src][:], T.meven[:], None, A.mult), [src, "meven"], ["xm0" + k])
-        V(192, lambda: ts(xm[:, :, 1, :], T[src][:], T.modd[:], None, A.mult), [src, "modd"], ["xm1" + k])
-        V(384, lambda: v.transpose(xt[:, :, :, :], xm[:, :, :, :]), ["xm0" + k, "xm1" + k], ["xt" + k])
-        V(384, lambda: tt(nm[:], xt[:, :, 0, :], xt[:, :, 1, :], A.add), ["xt" + k], ["nm" + k])
-
-    def lists(dst, src3, rk, wk):
-        for c in range(NL):
-            V(16, lambda c=c: v.tensor_copy(dst[:, c:W:NL], src3[:, c, :]), rk, [(wk, c)])
-
-    initial("e", "en")
-    for h in range(H):
-        lists(T.m0l[:, h], T.nme[:, NL * h:NL * h + NL, :], ["nme"], ("m0l", h))
-        if h == 0:
-            initial("s", "su")
-        lists(B("l0", h), T.nms[:, NL * h:NL * h + NL, :], ["nms"], ("l0", h))
-        if h == 0:
-            for n, val, d in IDENT:
-                if d == "float16":
-                    V(128, lambda n=n, val=val: ts(T[n][:], T.idf[:], val, None, A.mult), ["idf"], [n])
-                else:
-                    S(128, lambda n=n, val=val: act(T[n][:], T.idf[:], F.Copy, scale=val), ["idf"], [n])
-            for n, val in (("selc", 0.5), ("seld", 65536.0)):
-                V(80, lambda n=n: v.memset(T[n][:], 0.0), w=[n])
-                V(8, lambda n=n, val=val: ts(T[n][:, 15:143:16], T.g8c[:], val, None, A.mult), ["g8c"], [n])
-            V(W / 2, lambda: v.memset(T.kc8[:], 8.0), w=["kc8"])
-            for n, pat, base in (("krow", [[4096, 16], [0, NL]], 0), ("kkeep", [[0, NL], [256, 16]], -2048), ("kfill", [[0, NL], [256, 16]], 2048)):
-                op("g", 300, lambda n=n, pat=pat, base=base: g.iota(T[n][:], pat, base, 0, allow_small_or_imprecise_dtypes=True), w=[n])
-            for n, val in (("x17", 0.0), ("a17", 0), ("pb", 0)):
-                V(H * W17, lambda n=n, val=val: v.memset(T[n][:], val), w=[(n, q) for q in range(H)])
-            for n in ("mx", "mn"):
-                V(8, lambda n=n: v.memset(T[n][:, :, W17:W17 + 4], 0.0), w=[(n + "pad", q) for q in range(H)])
-            for n, base, at, val, m in (("rk17", 0.0, (0,), BIG, 17), ("mk17", 1.0, (0,), 0.0, 17), ("rm17", 0.0, (15, 16), -1.0e6, 17),
-                                        ("rn17", 0.0, (15, 16), 1.0e6, 17), ("tg17", 4096.0, (0,), -1.0e6, 17), ("kw", 2128.0, (15,), -1968.0, 17),
-                                        ("mk16", 1.0, (0,), 0.0, 16), ("rm16", 0.0, (15,), -1.0e6, 16)):
-                V(W17, lambda n=n, base=base: v.memset(T[n][:], base), w=[n])
-                for a in at:
-                    V(NL, lambda n=n, a=a, val=val, m=m: v.memset(T[n][:, a::m], val), w=[n])
     nloc = [0]
 
     def send(dst, land, out, in_, w, r):
         rid, pid = topo.addr(dst, core)
         m, ne = topo.mask(core, dst), len(topo.engines(core, dst))
         nloc[0] += ne
-        i = op("g", 300, lambda: [(g.remote_dma(out, in_, T.sem[land], T.sem.loc, pid, rid, m), None, 0)], r)
+        i = op("g", 150, lambda: [(g.remote_dma(out, in_, T.sem[land], T.sem.loc, pid, rid, m), None, 0)], r)
         j = op("r", 0, None, (), w, sem=land, val=ne, lat=RLAT)
         ops[j]["dep"].add(i)
 
-    send(opp, "ls2", T.ls2[:], T.m0l[:], ["ls2"], [(("m0l", h), c) for h in range(H) for c in range(NL)])
-    send(opp, "lsn2", T.lsn2[:], T.nme[:], ["lsn2"], ["nme"])
+    swk = [("swp", j, c) for j in range(2) for c in range(2)] + ["iph", "k2k"]
 
-    dn = [0]
-    pw = T.pw
+    def swapped(p, x, n):
+        return [(p[:, 0:n, :], T.iph[:], T.k2k[:, 0:16 * n], 16 * n)] + [
+            (p[:, j:n:2, :], T.swp[:, j, c, :], x[:, c:n:2, :], max(64, 8 * n)) for j in range(2) for c in range(2)]
+
+    dma("y", g.sync, T.en[:], T.enz[:], "lde", ["en"], 2000.0)
+    dma("s", g.scalar, T.su[:], T.subs[:], "lds", ["su"], 2000.0)
+    dma("y", g.sync, T.ct[:], T.cont[:], "ldc", ["ct"], 5700.0)
+
+    V(128, lambda: v.memset(T.one[:], 1.0), w=["one"])
+    op("g", 140, lambda: g.iota(T.pid[:], [[0, 1]], 0, 1), w=["pid"])
+    V(1, lambda: ts(T.pbit[:], T.pid[:], 16, None, A.bitwise_and), ["pid"], ["pbit"])
+    V(1, lambda: ts(T.modd[:], T.pbit[:], 1.0 / 16, None, A.mult), ["pbit"], ["modd"])
+    V(1, lambda: ts(T.meven[:], T.pbit[:], -1.0 / 16, 1.0, A.mult, A.add), ["pbit"], ["meven"])
+    for n, base in (("idf", 0), ("iup", 16), ("idn", -16)):
+        op("g", 380, lambda n=n, base=base: g.affine_select(T[n][:], T.one[:], [[-1, 128]], A.is_equal, 0.0, base, 1), ["one"], [n])
+    for j, c, n in ((0, 0, "idf"), (0, 1, "iup"), (1, 0, "idn"), (1, 1, "idf")):
+        m = ("meven", "modd")[j]
+        V(128, lambda j=j, c=c, n=n, m=m: ts(T.swp[:, j, c, :], T[n][:], T[m][:], None, A.mult), [n, m], [("swp", j, c)])
+    V(8, lambda: v.memset(T.g8a[:], 1.0), w=["g8a"])
+    op("g", 190, lambda: g.affine_select(T.g8b[:], T.g8a[:], [[-16, 8]], A.is_ge, 0.0, 0, 1), ["g8a"], ["g8b"])
+    op("g", 190, lambda: g.affine_select(T.g8c[:], T.g8b[:], [[16, 8]], A.is_ge, 0.0, 15, -1), ["g8b"], ["g8c"])
+    for n, val, d in IDENT:
+        if d == "float16":
+            V(128, lambda n=n, val=val: ts(T[n][:], T.idf[:], val, None, A.mult), ["idf"], [n])
+        else:
+            S(128, lambda n=n, val=val: act(T[n][:], T.idf[:], F.Copy, scale=val), ["idf"], [n])
+    V(96, lambda: v.memset(T.k2k[:], 2048.0), w=["k2k"])
+
+    for k, (src, l, nm) in enumerate((("en", "le1", "ne1"), ("su", "ls1", "ns1"))):
+        pn = "pd%d" % k
+        V(192, lambda k=k, src=src: ts(T.xf[:, k], T[src][:], -2048.0, None, A.add), [src], [("xf", k)])
+        V(96, lambda k=k: v.transpose(T.xt[:, k], T.xf[:, k]), [("xf", k)], [("xt", k)])
+        P(swapped(T[pn], T.xt[:, k], 12), [("xt", k)] + swk, [pn], [pn])
+        V(192, lambda pn=pn, l=l: v.tensor_copy(T[l][:], T[pn][:, 0:12, :]), [pn], [l], [pn])
+        S(192, lambda pn=pn, nm=nm: act(T[nm][:], T[pn][:, 0:12, :], F.Copy), [pn], [nm], [pn])
+    send(opp, "ls2", T.ls2[:], T.le1[:], ["ls2"], ["le1"])
+    send(opp, "ns2", T.ns2[:], T.ne1[:], ["ns2"], ["ne1"])
+    for n, val in (("selc", 1.0 if SIGNV else 0.5), ("seld", 16.0)):
+        V(80, lambda n=n: v.memset(T[n][:], 0.0), w=[n])
+        V(8, lambda n=n, val=val: ts(T[n][:, 15:143:16], T.g8c[:], val, None, A.mult), ["g8c"], [n])
+    op("g", 300, lambda: g.iota(T.krow[:], [[0, NL], [1, 16]], 0, 0, allow_small_or_imprecise_dtypes=True), w=["krow"])
+    for n, base, at, val, d in FILLS:
+        V(W / 2, lambda n=n, base=base: v.memset(T[n][:], base), w=[n])
+        if n in ("rm", "rn"):
+            V(W / 4, lambda n=n: v.memset(T[n][:, 1::2], 2.0), w=[n])
+        if at is not None:
+            V(NL, lambda n=n, at=at, val=val: v.memset(T[n][:, at::16], val), w=[n])
+    for a, val in enumerate((7044.0, 7072.0)):
+        V(W / 2, lambda a=a, val=val: v.memset(T.ku[:, a], val), w=["ku"])
+        V(NL, lambda a=a, val=val: v.memset(T.ku[:, a, 15::16], val - 8), w=["ku"])
+    for a, z, val in ((0, 2, 0.0), (2, 3, -192.0), (3, 4, 64.0 * 192 + 2048)):
+        V(W / 2, lambda a=a, z=z, val=val: v.memset(T.kt[:, a:z], val), w=["kt"])
+    for n in ("mx", "mn"):
+        V(16, lambda n=n: v.memset(T[n][:, :, W:W + 16], 0.0), w=[n + "pad"])
+
+    dn, later = [0], []
+
+    def chunk(t, h):
+        grp[0] = h
+        b = lambda n: T[n][:, h]
+        K = lambda *n: [(x, h) for x in n]
+        an, en_ = "pa%d" % ((t * H + h) % 2), "pe%d" % ((t * H + h) % 2)
+        reg = lambda p, i, n=1: T[p][:, i * W:(i + n) * W]
+        pC, pK, pX, pY = reg(an, 0), reg(en_, 0), reg(en_, 1), reg(en_, 2)
+        ws = slice(W * h, W * h + W)
+        el, ek = (T.le1[:, ws], ["le1"]) if t == 1 else (b("le%d" % t), K("le%d" % t))
+        sl, sk, zn, znk = (T["ls%d" % t][:, ws], ["ls%d" % t], T["ns%d" % t][:, ws], ["ns%d" % t]) if t < 3 else (b("ls3"), K("ls3"), b("ns3"), K("ns3"))
+
+        def gather(n, l, lk):
+            for c in range(NL):
+                o, x = b(n)[:, c], T.ct[:].indirect(l[:, 16 * c:16 * c + 16])
+                if c >= NL - GV.get((t, h, n), 0):
+                    V(256 * GA, lambda o=o, x=x: v.tensor_copy(o, x), ["ct"] + lk, [(n, h, c)])
+                else:
+                    S(256 * GA, lambda o=o, x=x: act(o, x, F.Copy), ["ct"] + lk, [(n, h, c)])
+            return [(n, h, c) for c in range(NL)]
+        vk = gather("v", el, ek)
+        yk = gather("y", sl, sk)
+        x, y = b("v"), b("y")
+        for c in range(0, NL, 2):
+            pn = "pd%d" % (dn[0] % NDIFF); dn[0] += 1
+            p, o, xk = T[pn], b("sg")[:, c:c + 2], [("v", h, c), ("v", h, c + 1)]
+            turned = lambda m: [(p[:, 0:15, :], m, x[:, c, 16:256], 240), (p[:, 16:31, :], m, x[:, c + 1, 16:256], 240), (p[:, 15::16, :], m, x[:, c:c + 2, 0:16], 64)]
+            if SIGNV:
+                for z in turned(T.ip[:]): P([z], xk + ["ip"], [pn], [pn])
+                V(512, lambda p=p, o=o, c=c: tt(o, x[:, c:c + 2], p[:], A.is_gt), [pn] + xk, [("sg", h, c)], [pn])
+            else:
+                P([(p[:], T.ip[:], x[:, c:c + 2], 512)] + turned(T.im[:]), xk + ["ip", "im"], [pn], [pn])
+                S(512, lambda p=p, o=o: act(o, p[:], F.Sign, bias=-0.5), [pn], [("sg", h, c)], [pn])
+        for r in range(0, 16, RB):
+            pn = "pd%d" % (dn[0] % NDIFF); dn[0] += 1
+            p = T[pn]
+            P([(p[:, 0:NL * RB, :], T.ip[:], y[:, :, 16 * r:16 * (r + RB)], W * RB)] + [(p[:, i:NL * RB:RB, :], T.im[:], x[:, :, 240:256], W) for i in range(RB)],
+              vk + yk + ["ip", "im"], [pn], [pn])
+            S(W * RB, lambda p=p, o=b("ab")[:, :, r:r + RB]: act(o, p[:, 0:NL * RB, :], F.Abs), [pn], [("ab", h, r)], [pn])
+
+        def sums(p, first, sel, z, r, w, bank):
+            P(first, r[0], w, bank, stop=False)
+            for a in range(0, 16, 4):
+                P([(p, sel[:, 15 - m:143 - m], z[:, :, :, m], W) for m in range(a, a + 4)], r[1], w, bank, start=False, stop=a == 12)
+        more = [(pC, T.iph[:], T.kc1[:], W)] if t == 1 else [(pC, T.iph[:], T.kc2[:], W), (pC, T.ia[:], b("nb"), W), (pC, T.ib[:], b("hn"), W)]
+        sums(pC, more, T.selc, b("sg"), (["iph", "kc1", "kc2", "ia", "ib"] + K("nb", "hn"), [("sg", h, c) for c in range(0, NL, 2)] + ["selc"]), [an + "C", an + "T"], [an])
+        sums(pK, [(pK, T.ip[:], T.krow[:], W)], T.seld, b("ab"), (["ip", "krow"], [("ab", h, r) for r in range(0, 16, RB)] + ["seld"]), [en_ + "K"], [en_])
+        while later: later.pop()()
+        grp[0] = h
+        V(W, lambda: scan(b("cc"), T.mk[:], pC, 0.0, A.mult, A.add), [an + "C", "mk"], K("cc"), [an])
+        S(W, lambda: act(b("w"), pC, F.Sign, bias=-9.5), [an + "C"], K("w"), [an])
+        S(W, lambda: act(b("u"), pC, F.Sign, bias=5.5 if t == 1 else 6.0 + 1.0 / 256, scale=-1.0), [an + "C"], K("u"), [an])
+        V(W, lambda: ts(b("par"), b("cc"), 1, None, A.bitwise_and), K("cc"), K("par"))
+        for e in range(2):
+            V(W / 2, lambda e=e: ts(b("st")[:, e::2], b("par")[:, e::2], -2.0, 2.0 * e - 1.0, A.mult, A.add), K("par"), K("st%d" % e))
+        V(W, lambda: scan(b("km"), T.rk[:], pK, 0.0, A.add, A.min), [en_ + "K", "rk"], K("km"), [en_])
+        V(NL, lambda: ts(b("st")[:, 0::16], b("km")[:, 15::16], 15, None, A.bitwise_and), K("km"), K("st0"))
+        V(W, lambda: scan(b("pos"), T.mk[:], b("st"), 0.0, A.mult, A.add), K("st0", "st1") + ["mk"], K("pos"))
+        V(W / 2, lambda: scan(b("mx")[:, W - 1::-1], T.rm[:, ::-1], b("pos")[:, ::-1], 0.0, A.add, A.max), K("pos") + ["rm"], K("mx"))
+        V(W / 2, lambda: scan(b("mn")[:, W - 1::-1], T.rn[:, ::-1], b("pos")[:, ::-1], 0.0, A.add, A.min), K("pos") + ["rn"], K("mn"))
+        affine("H", W, True, b("hp"), b("pos"), 0.5, 191.75, K("pos"), K("hp"))
+        affine("F", W, True, b("fp"), b("pos"), 1.0 / 16, 136.0 - 15.0 / 32, K("pos"), K("fp"))
+        affine("h", W, True, b("hs"), el, 1.0 / 64, 192.0 - 63.0 / 128, ek, K("hs"))
+        affine("h", W, True, b("sh"), el, 1.0, -2048.0, ek, K("sh"))
+        mx, mn, it = b("mx"), b("mn"), T["it%d" % t]
+        pA, pB, qp = reg(an, 0), reg(an, 1), b("qp")
+        two = lambda f: [z for p in ((pA, pB) if TWICE else (pA,)) for z in f(p)]
+        low = lambda p: [(p, T.im63[:], b("hs"), W), (p, T.iph[:], b("sh"), W), (p, it[:], b("w"), W), (p, it[:], T.k1[:], W)]
+        lowk = K("hs", "sh", "w") + ["im63", "iph", "k1", "it%d" % t]
+        if TWICE:
+            P([(reg(an, 0, 2), T.iKh[:], T.ku[:], 2 * W), (pA, T.ip[:], b("hs"), W)] + low(pB) + two(lambda p: [(p, T.iw[:], b("w"), W), (p, T.iu[:], b("u"), W)]),
+              K("u") + lowk + ["iKh", "ku", "iw", "iu", "ip"], [an + "C"], [an], stop=False)
+        else:
+            P([(pA, T.iKh[:], T.ku[:, 0], W), (pA, T.iw[:], b("w"), W), (pA, T.iu[:], b("u"), W)], K("u", "w") + ["iKh", "ku", "iw", "iu"], [an + "C"], [an], stop=False)
+            P([(pY, T.iKh[:], T.k28[:], W)] + low(pY), lowk + ["iKh", "k28"], [en_ + "Y"], [en_])
+            affine("lo", W, False, b("lo"), pY, 1.0, 0.0, [en_ + "Y"], K("lo"), [en_])
+        P(two(lambda p: [(p, T.ip16[:], b("pos"), W)]), K("pos") + ["ip16"], [an + "C"], [an], start=False, stop=False)
+        P(two(lambda p: [(p, T.im8[:], mx[:, 0:W], W), (p, T.ip8[:], mx[:, 1:W + 1], W), (p[:, 15::16], T.im8[:], mx[:, 16:W + 1:16], 64)]),
+          K("mx") + ["mxpad", "im8", "ip8"], [an + "C"], [an], start=False, stop=False)
+        P(two(lambda p: [(p, T.ip8[:], mn[:, 0:W], W), (p, T.im8[:], mn[:, 1:W + 1], W), (p[:, 15::16], T.ip8[:], mn[:, 16:W + 1:16], 64)]),
+          K("mn") + ["mnpad", "im8", "ip8"], [an + "C"], [an], start=False, stop=False)
+        P(two(lambda p: [(p, T.iH[:], b("hp"), W), (p, T.im8[:], b("fp"), W)]), K("hp", "fp") + ["iH", "im8"], [an + "C"], [an], start=False)
+        if TWICE:
+            qe, qek = reg(an, 0, 2)[:, 0::2], [an + "C"]
+            affine("B", W, False, b("qb"), reg(an, 0, 2)[:, 1::2], 1.0, 0.0, [an + "C"], K("qb0", "qb1"), [an])
+        else:
+            qe, qek = reg(an, 1), [an + "Q0", an + "Q1"]
+            for a, n in enumerate(("hs", "lo")):
+                V(W / 2, lambda a=a, n=n: tt(b("qb")[:, a], pA[:, 1::2], b(n)[:, 1::2], A.add), [an + "C"] + K(n), K("qb%d" % a), [an])
+                V(W / 2, lambda a=a, n=n: tt(qe[:, a * W // 2:(a + 1) * W // 2], pA[:, 0::2], b(n)[:, 0::2], A.add), [an + "C"] + K(n), [an + "Q%d" % a], [an])
+        V(W, lambda: tt(b("qx"), qe, b("qb"), A.max), qek + K("qb0", "qb1"), K("qx"), [an])
+        V(W, lambda: tt(qp[:, :, :, 8:16, 0], qe, b("qb"), A.min), qek + K("qb0", "qb1"), K("qpe"), [an])
+        V(W, lambda: ts(qp[:, :, :, 8:16, 1], b("qx"), -16 * KEY, None, A.add), K("qx"), K("qpo"))
+        V(14 * NL, lambda: v.tensor_copy(qp[:, :, :, 1:8, :], qp[:, :, :, 9:16, :]), K("qpe", "qpo"), K("qpd"))
+        tk = [an + "T"]
+        P([(reg(an, 1, 4), T.ip[:], T.kt[:], 4 * W), (reg(an, 3), T.ip[:], b("hs"), W), (reg(an, 4), T.im64[:], b("hs"), W), (reg(an, 4), T.iph[:], b("sh"), W)],
+          K("hs", "sh") + ["ip", "kt", "im64", "iph", an + "C"], tk, [an], stop=False)
+        for a, z in zip(ESPLIT, ESPLIT[1:]):
+            for d in range(a, z):
+                V(W, lambda d=d: ts(b("o1")[:, d], qp[:, :, :, 8 - d:16 - d, :], KEY * (d - 4), KEY * (d - 3), A.max, A.min), K("qpe", "qpo") + (K("qpd") if d else []), [("o1", h, d)])
+            P([(pX, c[:], b("o1")[:, d, e], W) for d in range(a, z) for e, c in ((0, T.i63h), (1, T.iph))], [("o1", h, d) for d in range(a, z)] + ["i63h", "iph"],
+              [en_ + "X", en_ + "Y"], [en_], start=a == 0, stop=z == 8)
+        V(W, lambda: v.tensor_copy(b("ei"), pX), [en_ + "X"], K("ei"), [en_])
+        V(W, lambda: ts(b("xx"), b("ei"), 32767, None, A.bitwise_and), K("ei"), K("xx"))
+        V(W, lambda: ts(b("dl"), b("xx"), 14336.0, None, A.is_ge), K("xx"), K("dl"))
+        V(W / 2, lambda: scan(b("ii"), T.mk[:], b("dl"), 0.0, A.mult, A.add), K("dl") + ["mk"], K("ii"))
+        V(W / 2, lambda: scan(b("nb")[:, ::-1], T.rz[:, ::-1], b("ii")[:, ::-1], 0.0, A.add, A.max), K("ii") + ["rz"], K("nb"))
+        P([(reg(an, a), m[:], b(n), W) for a in (1, 2) for m, n in ((T.ip8, "dl"), (T.i64, "ii"))], K("dl", "ii") + ["ip8", "i64"], tk, [an], start=False, stop=False)
+        P([(reg(an, a), T.i64[:], b("nb"), W) for a in (3, 4)], K("nb") + ["i64"], tk, [an], start=False)
+        V(W, lambda: ts(b("n32"), b("xx"), 2048.0, 32.0, A.is_lt, A.mult), K("xx"), K("n32"))
+        V(W, lambda: ts(pY, b("xx"), -8192.0 - 77 * t, 0.0, A.add, A.max), K("xx"), [en_ + "Y"], [en_])
+        V(W, lambda: tt(pY, pY, b("n32"), A.add), K("n32"), [en_ + "Y"], [en_])
+        V(W, lambda: tt(b("az"), pY, zn, A.mult), [en_ + "Y"] + znk, K("az"), [en_])
+        V(W, lambda: ts(b("sf"), b("az"), 5, 4095, A.arith_shift_right, A.bitwise_and), K("az"), K("sf"))
+        V(W, lambda: tt(b("b2"), pX, b("sf"), A.add), [en_ + "X"] + K("sf"), K("b2"), [en_])
+        V(W, lambda: ts(b("n2")[:, 0], b("b2"), 6, 63, A.arith_shift_right, A.bitwise_and), K("b2"), K("n2h"))
+        V(W, lambda: ts(b("n2")[:, 1], b("b2"), 63, None, A.bitwise_and), K("b2"), K("n2l"))
+        q2, o2 = b("q2"), b("o2")
+        V(2 * W, lambda: v.tensor_copy(q2[:, :, :, 16:32], reg(an, 3, 2)), tk, K("q2b"), [an])
+        V(2 * W, lambda: tt(q2[:, :, :, 0:16], reg(an, 1, 2), b("n2"), A.add), tk + K("n2h", "n2l"), K("q2a"), [an])
+        P([(pK, T.iR[:], T.kres[:], W), (pK, T.iR[:], b("nb"), W)], K("nb") + ["iR", "kres"], [en_ + "K", en_ + "X"], [en_], stop=False)
+        for a, z in zip(RSPLIT, RSPLIT[1:]):
+            for d in range(a, z):
+                d = 16 - d
+                V(W, lambda d=d: ts(o2[:, d], q2[:, :, :, d:d + 16], 64.0 * d, 64.0 * d + 64.0, A.max, A.min), K("q2b") + (K("q2a") if d < 16 else []), [("o2", h, d)])
+            P([(pK, c[:], o2[:, 16 - d, e], W) for d in range(a, z) for e, c in ((0, T.i64h), (1, T.iph))],
+              [("o2", h, 16 - d) for d in range(a, z)] + ["iph", "i64h"], [en_ + "K"], [en_], start=False, stop=z == 17)
+        if t < R:
+            n = t + 1
+            ml, mk = b("ml%d" % t), K("ml%d" % t)
+            V(W, lambda: v.tensor_copy(ml, pK), [en_ + "K"], mk, [en_])
+            send(nxt, "le%d%d" % (n, h), b("le%d" % n), ml, K("le%d" % n), mk)
+            if t + 2 <= R:
+                affine("nm", W, False, b("nm"), pK, 1.0, 0.0, [en_ + "K"], K("nm"), [en_])
+                send(prv, "ls3%d" % h, b("ls3"), ml, K("ls3"), mk)
+                send(prv, "ns3%d" % h, b("ns3"), b("nm"), K("ns3"), K("nm"))
+            affine("hn", W, True, b("hn"), b("nb"), 0.5, 135.75, K("nb"), K("hn"))
+        if t >= R - 1:
+            V(W, lambda: ts(b("nh"), pK, -2048.0, None, A.add), [en_ + "K"], K("nh"), [en_])
+
+        def result():
+            grp[0] = h
+            pn = "pd%d" % (dn[0] % NDIFF); dn[0] += 1
+            P(swapped(T[pn], b("nh"), NL), K("nh") + swk, [pn], [pn])
+            V(W, lambda: v.transpose(b("yo%d" % t), T[pn][:, 0:NL, :]), [pn], K("yo%d" % t), [pn])
+            send(nxt if t == R else prv, "ly%d%d" % (t, h), b("ly%d" % t), b("yo%d" % t), K("ly%d" % t), K("yo%d" % t))
+            y_ = T.yenz if t == R else T.ysub
+            op("y", 60, lambda: [(g.sync.dma_start(y_[:, ws], b("ly%d" % t)), "out", 16)], K("ly%d" % t), lat=2000.0)
+        if t >= R - 1: later.append(result)
+
     for t in range(1, R + 1):
         for h in range(H):
-            b = lambda n: B(n, h)
-            K = lambda *n: [(x, h) for x in n]
-            eb = "pe%d" % ((t * H + h) % 2)
-            pE = T[eb]
-            ck = T.pck[:, h % CKS, :, :, 0:NL]
-            w0, w1 = pw[:, 2 * h, 0:W], pw[:, 2 * h + 1, 0:W]
-            k0, k1 = [("pw", 2 * h)], [("pw", 2 * h + 1)]
-            cs = slice(NL * h, NL * h + NL)
-            if t == 1:
-                el, ek = T.m0l[:, h], [(("m0l", h), c) for c in range(NL)]
-                sl, sk = b("l0"), [(("l0", h), c) for c in range(NL)]
-                en, enk, zn, znk = T.nme[:, cs, :], ["nme"], T.nms[:, cs, :], ["nms"]
-            else:
-                el, ek, en, enk = b("le%d" % t), K("le%d" % t), b("len%d" % t), K("len%d" % t)
-                if t == 2:
-                    sl, sk, zn, znk = T.ls2[:, h], ["ls2"], T.lsn2[:, cs, :], ["lsn2"]
-                else:
-                    sl, sk, zn, znk = b("ls3"), K("ls3"), b("lsn3"), K("lsn3")
-            def gather(n, l, lk, a, z):
-                for c in range(a, z, 64):
-                    e = min(c + 64, z)
-                    S(16 * (e - c) * 1.55, lambda c=c, e=e, y=b(n): act(y[:, 16 * (c - a):16 * (e - a)], T.ct[:].indirect(l[:, c:e]), F.Copy), ["ct"] + lk, [(n, h, c)])
-                return [(n, h, c) for c in range(a, z, 64)]
-            v15k = gather("v15", el, ek, W - NL, W)
-            yk = gather("y", sl, sk, 0, W)
-            for q in range(len(yk)): ops[-1 - q]["late"] = True
-            vk = gather("v", el, ek, 0, W)
-
-            def vdiff(q, p, x):
-                a = PC * q
-                mm(p[:, 0:PC], T.ip[:], x[:, a:a + PC], True, False)
-                if q < NP - 1:
-                    return mm(p[:, 0:PC], T.im[:], x[:, a + W:a + W + PC], False, True)
-                mm(p[:, 0:PC - W], T.im[:], x[:, a + W:NV], False, False)
-                return mm(p[:, PC - W:PC], T.im[:], x[:, 0:W], False, True)
-
-            def ydiff(q, p, y, x):
-                mm(p[:, 0:PC], T.ip[:], y[:, PC * q:PC * q + PC], True, False)
-                for i in range(RP):
-                    z = mm(p[:, W * i:W * i + W], T.im[:], x[:], False, i == RP - 1)
-                return z
-
-            def sums(p, sel, x, con):
-                for m in range(16):
-                    mm(p, sel[:, 15 - m:143 - m], x[:, m:NV:16], m == 0, False)
-                return mm(p, T.ip[:], con[:], False, True)
-
-            for kind in (1, 0):
-                for q in range(NP):
-                    pn = "pd%d" % (dn[0] % NDIFF); dn[0] += 1
-                    a, z = PC * q, PC * q + PC
-                    if kind == 0:
-                        P(2 * PC, lambda q=q, p=T[pn], x=b("v"), f=vdiff: f(q, p, x), vk + ["ip", "im"], [pn], [pn])
-                        S(PC, lambda a=a, z=z, p=T[pn], o=b("sg"): act(o[:, a:z], p[:, 0:PC], F.Sign, bias=-0.5), [pn], [("sg", h, q)], [pn])
-                    else:
-                        P(2 * PC, lambda q=q, p=T[pn], y=b("y"), x=b("v15"), f=ydiff: f(q, p, y, x), v15k + yk + ["ip", "im"], [pn], [pn])
-                        S(PC, lambda a=a, z=z, p=T[pn], o=b("ab"): act(o[:, a:z], p[:, 0:PC], F.Abs), [pn], [("ab", h, q)], [pn])
-            P(17 * W, lambda p=ck[:, 1], x=b("ab"), f=sums: f(p, T.seld, x, T.krow), [("ab", h, q) for q in range(NP)] + ["seld", "ip", "krow"], K("pk"), ["pck"])
-            P(17 * W, lambda p=ck[:, 0], x=b("sg"), f=sums: f(p, T.selc, x, T.kc8), [("sg", h, q) for q in range(NP)] + ["selc", "ip", "kc8"], K("pc"), ["pck"])
-            for c in range(NL):
-                S(32, lambda c=c, p=ck, x=b("x17"): act(x[:, :, 17 * c:17 * c + 16], p[:, :, :, c], F.Copy), K("pc", "pk"), [("x17", h, c)], ["pck"])
-            x17k = [("x17", h)] + [("x17", h, c) for c in range(NL)]
-            V(W, lambda o=b("s2"), x=en: ts(o[:, 0, :, :], x[:], 7, None, A.arith_shift_right), enk, K("s2h"))
-            V(W, lambda o=b("sl"), x=en: ts(o[:], x[:], 127, None, A.bitwise_and), enk, K("sl"))
-            V(2 * W, lambda o=b("s2"), x=b("sl"): tt(o[:, 1, :, :], x[:], o[:, 0, :, :], A.add), K("sl", "s2h"), K("s2l"))
-            V(W17, lambda x=b("x17"), o=b("cc"): scan(o[:], T.mk17[:], x[:, 0, :], 0.0, A.mult, A.add), x17k + ["mk17"], K("cc"))
-            V(W17, lambda x=b("x17"), o=b("km"): scan(o[:], T.rk17[:], x[:, 1, :], 0.0, A.add, A.min), x17k + ["rk17"], K("km"))
-            V(W17, lambda x=b("cc"), o=b("par"): ts(o[:], x[:], 1, None, A.bitwise_and), K("cc"), K("par"))
-            V(NL, lambda x=b("km"), o=b("pb"): ts(o[:, 0::17], x[:, 15::17], 4096, None, A.bitwise_and), K("km"), K("pb"))
-            V(W17, lambda x=b("par"), o=b("st"): ts(o[:], x[:], -8192.0, 4096.0, A.mult, A.add), K("par"), K("st"))
-            V(W17, lambda x=b("pb"), o=b("od"): scan(o[:], T.tg17[:], x[:], 0.0, A.subtract, A.max), K("pb") + ["tg17"], K("od"))
-            V(NL, lambda x=b("km"), o=b("st"): ts(o[:, 0::17], x[:, 15::17], 61440, None, A.bitwise_and), K("km"), K("st"))
-            V(W17, lambda x=b("st"), o=b("pos"): scan(o[:], T.mk17[:], x[:], 0.0, A.mult, A.add), K("st") + ["mk17"], K("pos"))
-            V(W17, lambda x=b("pos"), o=b("mx"): scan(o[:, W17 - 1::-1], T.rm17[:, ::-1], x[:, ::-1], 0.0, A.add, A.max), K("pos") + ["rm17"], K("mx"))
-            V(W17, lambda x=b("pos"), o=b("mn"): scan(o[:, W17 - 1::-1], T.rn17[:, ::-1], x[:, ::-1], 0.0, A.add, A.min), K("pos") + ["rn17"], K("mn"))
-            S(W17, lambda x=b("pos"), o=b("g1"): act(o[:], x[:], F.Sign, bias=63488.0, scale=-1.0), K("pos"), K("g1"))
-            S(W17, lambda x=b("pos"), o=b("g2"): act(o[:], x[:], F.Sign, bias=-2048.0, scale=-1.0), K("pos"), K("g2"))
-            S(W17, lambda x=b("x17"), o=b("w"): act(o[:], x[:, 0, :], F.Sign, bias=-9.5), x17k, K("w"))
-            if t > 1:
-                V(2 * W17, lambda x=b("x17"), o=b("d1"), a=b("a17"): tt(o[:], x[:, 0, :], a[:], A.subtract), x17k + K("a17"), K("d1"))
-            dk, dx = (K("d1"), b("d1")) if t > 1 else (x17k, b("x17")[:, 0, :])
-            S(W17, lambda x=dx, o=b("u"): act(o[:], x[:], F.Sign, bias=5.5, scale=-1.0), dk, K("u"))
-
-            def usum(p, h):
-                o = p[:, 0:NL, 32:49]
-                mm(o, T.ip[:], T.kw[:], True, False)
-                for n, c in (("od", "i4"), ("w", "i16"), ("u", "i32"), ("pos", "i16th"), ("g1", "i2048"), ("g2", "i2048")):
-                    mm(o, T[c][:], B(n, h)[:], False, False)
-                mm(o, T.im[:], B("mx", h)[:, 0:W17], False, False)
-                mm(o, T.ip[:], B("mx", h)[:, 1:W17 + 1], False, False)
-                mm(o, T.ip[:], B("mn", h)[:, 0:W17], False, False)
-                return mm(o, T.im[:], B("mn", h)[:, 1:W17 + 1], False, True)
-            P(11 * W17, lambda p=pE, h=h: usum(p, h), K("od", "pos", "g1", "g2", "u", "w", "mx", "mn", "mxpad", "mnpad") + ["ip", "im", "i16th", "i16", "i4", "i32", "i2048", "kw"], ["U" + eb], [eb])
-            for a, sk2 in ((0, "s2h"), (1, "s2l")):
-                V(W, lambda a=a, o=b("q1"), x=b("s2"), p=pE: tt(o[:, a, :, :], x[:, a, :, :], p[:, 0:NL, 32:48], A.add), K(sk2) + ["U" + eb], K("q1%d" % a), [eb])
-            V(2 * W, lambda o=b("qx"), x=b("q1"): tt(o[:], x[:, :, :, 0::2], x[:, :, :, 1::2], A.max), K("q10", "q11"), K("qx"))
-            V(2 * W, lambda o=b("qp"), x=b("q1"): tt(o[:, :, :, 0, :], x[:, :, :, 0::2], x[:, :, :, 1::2], A.min), K("q10", "q11"), K("qpe"))
-            V(W, lambda o=b("qp"), x=b("qx"): ts(o[:, :, :, 1, :], x[:], -16640.0, None, A.add), K("qx"), K("qpo"))
-            for p_ in range(8):
-                V(W, lambda p_=p_, o=b("o1"), x=b("qp"): ts(o[:, :, :, p_, :, :], x[:], 512.0 * p_ - 2048.0, 512.0 * p_ - 1792.0, A.max, A.min), K("qpe", "qpo"), [("o1", h, p_)])
-
-            def picked(p, q, o, n, f):
-                for k in range(n):
-                    for a, c in ((0, T.i127h), (1, T.iph)):
-                        x = o[:, a, :, 8 * f:8 * f + 8, k] if n == 17 else o[:, a, :, 4 * f:4 * f + 4, :, k]
-                        z = mm(p[:, 0:NL, q + 8 * f:q + 8 * f + 8], c[:], x, k == 0 and a == 0, k == n - 1 and a == 1)
-                return z
-            for f in range(2):
-                P(16 * max(64, W // 2), lambda p=pE, o=b("o1"), f=f, pk=picked: pk(p, 0, o, 8, f), [("o1", h, p_) for p_ in range(4 * f, 4 * f + 4)] + ["iph", "i127h"], ["E%d" % f + eb], [eb])
-            V(W, lambda o=b("ei"), p=pE: v.tensor_copy(o[:], p[:, 0:NL, 0:16]), ["E0" + eb, "E1" + eb], K("ei"), [eb])
-            V(W, lambda o=b("xx"), x=b("ei"): ts(o[:], x[:], 16383, None, A.bitwise_and), K("ei"), K("xx"))
-            V(W, lambda x=b("xx"), o=b("dl"): ts(o[:], x[:], 12288.0, None, A.is_ge), K("xx"), K("dl"))
-            V(W, lambda x=b("dl"), o=b("ii"): scan(o[:], T.mk16[:], x[:], 0.0, A.mult, A.add), K("dl") + ["mk16"], K("ii"))
-            V(W, lambda x=b("ii"), o=b("nb"): scan(o[:, ::-1], T.rm16[:, ::-1], x[:, ::-1], 0.0, A.add, A.max), K("ii") + ["rm16"], K("nb"))
-
-            def tsum(p, h):
-                o = p[:, 0:NL, 32:48]
-                mm(o, T.ip[:], T.kkeep[:], True, False)
-                mm(o, T.i8192[:], B("dl", h)[:], False, False)
-                mm(o, T.im256[:], B("ii", h)[:], False, True)
-                o = p[:, 0:NL, 0:16]
-                mm(o, T.ip[:], T.kfill[:], True, False)
-                return mm(o, T.im256[:], B("nb", h)[:], False, True)
-            P(5 * W, lambda p=pE, h=h: tsum(p, h), K("dl", "ii", "nb") + ["i8192", "im256", "ip", "kkeep", "kfill"], ["T" + eb, "U" + eb, "E0" + eb, "E1" + eb], [eb])
-            V(W, lambda x=b("xx"), o=w0: ts(o, x[:], -8192.0, 0.0, A.add, A.max), K("xx"), k0)
-            V(W, lambda x=b("xx"), o=b("n32"): ts(o[:], x[:], 4096.0, 32.0, A.is_lt, A.mult), K("xx"), K("n32"))
-            V(W, lambda x=b("xx"), o=w1, t=t: ts(o, x[:], 8192.0, 77.0 * t, A.is_ge, A.mult), K("xx"), k1)
-            V(W, lambda x=b("n32"), o=w0: tt(o, x[:], o, A.add), K("n32"), k0)
-            V(W, lambda x=b("xx"), o=w1: tt(o, x[:], o, A.add), K("xx"), k1)
-            V(W, lambda x=zn, o=b("az"), y=w0: tt(o[:], x, y, A.mult), znk + k0, K("az"))
-            V(W, lambda x=b("az"), o=b("sf"): ts(o[:], x[:], 5, 4095, A.arith_shift_right, A.bitwise_and), K("az"), K("sf"))
-            V(W, lambda x=b("sf"), o=b("b2"), y=w1: tt(o[:], x[:], y, A.add), K("sf") + k1, K("b2"))
-            V(W, lambda x=b("b2"), o=b("n2"): ts(o[:, 0, :], x[:], 7, 31, A.arith_shift_right, A.bitwise_and), K("b2"), K("n2h"))
-            V(W, lambda x=b("b2"), o=b("n2"): ts(o[:, 1, :], x[:], 127, None, A.bitwise_and), K("b2"), K("n2l"))
-            for a, sk2 in ((0, "s2h"), (1, "s2l")):
-                V(W, lambda a=a, o=b("q2"), x=b("s2"), p=pE: tt(o[:, a, :, 16:32], x[:, a, :, :], p[:, 0:NL, 0:16], A.add), K(sk2) + ["T" + eb], K("q2b%d" % a), [eb])
-            V(W, lambda x=b("n2"), p=pE, o=w0: tt(o, x[:, 0, :], p[:, 0:NL, 32:48], A.add), K("n2h") + ["T" + eb], k0, [eb])
-            V(W, lambda x=b("n2"), o=b("q2"), y=w0: tt(o[:, 1, :, 0:16], x[:, 1, :], y, A.add), K("n2l") + k0, K("q2a1"))
-            V(W, lambda o=b("q2"), y=w0: v.tensor_copy(o[:, 0, :, 0:16], y), k0, K("q2a0"))
-            for i in range(16):
-                V(W17, lambda i=i, o=b("o2"), x=b("q2"): ts(o[:, :, :, i, :], x[:, :, :, i:i + 17], 256.0 * i - 2048.0, 256.0 * i - 1792.0, A.max, A.min), K("q2a0", "q2a1", "q2b0", "q2b1"), [("o2", h, i)])
-            for f in range(2):
-                P(34 * max(64, W // 2), lambda p=pE, o=b("o2"), f=f, pk=picked: pk(p, 16, o, 17, f), [("o2", h, i) for i in range(8 * f, 8 * f + 8)] + ["iph", "i127h"], ["R%d" % f + eb], [eb])
-            nm, nmk = b("nm%d" % t), K("nm%d" % t)
-            V(W, lambda o=b("fi"), p=pE: v.tensor_copy(o[:], p[:, 0:NL, 16:32]), ["R0" + eb, "R1" + eb], K("fi"), [eb])
-            V(W, lambda o=nm, x=b("fi"): ts(o[:], x[:], 4095, None, A.bitwise_and), K("fi"), nmk)
-            if t < R:
-                n = t + 1
-                lists(b("ml%d" % t), nm, nmk, ("ml%d" % t, h))
-                mk = [(("ml%d" % t, h), c) for c in range(NL)]
-                send(nxt, "le%d%d" % (n, h), b("le%d" % n)[:], b("ml%d" % t)[:], K("le%d" % n), mk)
-                send(nxt, "len%d%d" % (n, h), b("len%d" % n)[:], nm[:], K("len%d" % n), nmk)
-                if t + 2 <= R:
-                    send(prv, "ls3%d" % h, b("ls3")[:], b("ml%d" % t)[:], K("ls3"), mk)
-                    send(prv, "lsn3%d" % h, b("lsn3")[:], nm[:], K("lsn3"), nmk)
-                V(W, lambda x=b("nb"), o=b("ni"): v.tensor_copy(o[:], x[:]), K("nb"), K("ni"))
-                V(W, lambda x=b("ni"), o=b("a17"): ts(o[:, :, 0:16], x[:], 1, None, A.bitwise_and), K("ni"), K("a17"))
-            if t >= R - 1:
-                V(W, lambda x=nm, o=b("tm"): ts(o[:, :, 0, :], x[:], T.meven[:], None, A.mult), nmk + ["meven"], K("tm0"))
-                V(W, lambda x=nm, o=b("tm"): ts(o[:, :, 1, :], x[:], T.modd[:], None, A.mult), nmk + ["modd"], K("tm1"))
-                V(2 * W, lambda x=b("tm"), o=b("tt"): v.transpose(o[:], x[:]), K("tm0", "tm1"), K("tt"))
-                V(2 * W, lambda x=b("tt"), o=b("yo%d" % t): tt(o[:], x[:, :, 0, :], x[:, :, 1, :], A.add), K("tt"), K("yo%d" % t))
-                send(nxt if t == R else prv, "ly%d%d" % (t, h), b("ly%d" % t)[:], b("yo%d" % t)[:], K("ly%d" % t), K("yo%d" % t))
-                y = T.yenz if t == R else T.ysub
-                op("y", 60, lambda y=y, x=b("ly%d" % t), h=h: [(g.sync.dma_start(y[:, W * h:W * h + W], x[:]), "out", 16)], K("ly%d" % t))
+            chunk(t, h)
+    for f in later: f()
 
     n = len(ops)
+    pred = [sorted(o["dep"]) for o in ops]
     succ = [[] for i in range(n)]
-    for i, o in enumerate(ops):
-        for d in o["dep"]: succ[d].append(i)
-        o["pr"] = i + (LATE if o.get("late") else 0)
-    by_pr = sorted(range(n), key=lambda i: ops[i]["pr"])
+    for i in range(n):
+        for d in pred[i]: succ[d].append(i)
+    gap = lambda i, j: ops[i]["lat"] + (0.0 if ops[i]["eng"] == "p" and ops[j].get("adds") else WAKE)
 
-    def schedule(known):
-        left = [len(o["dep"]) for o in ops]
-        ready = [0.0] * n
-        free, order, cand, urgent, out = {}, [], {}, {}, set()
-        if known:
-            for i in by_pr: urgent.setdefault(ops[i]["eng"], []).append(i)
-        end = 0.0
-        for i in range(n):
-            if not left[i]: cand.setdefault(ops[i]["eng"], []).append(i)
-        while True:
-            best = None
-            for e, c in cand.items():
-                if not c: continue
-                f = free.get(e, 0.0) if e != "r" else 0.0
-                starts = []
-                for i in c:
-                    st = max(ready[i], f)
-                    if known and ops[i]["cost"] > HOLD:
-                        lim = st + AHEAD * ops[i]["cost"]
-                        for j in urgent[e]:
-                            if ops[j]["pr"] >= ops[i]["pr"]: break
-                            if j not in out and left[j] and st < known[j] < lim: st = known[j] + 1.0
-                    starts.append((st, i))
-                lo = min(starts)[0]
-                pr, st, i = min((ops[i]["pr"], st, i) for st, i in starts if st <= lo + 20.0)
-                if best is None or (st, i) < best[0]: best = ((st, i), e, i)
-            if best is None: break
-            (st, _), e, i = best
-            cand[e].remove(i)
-            out.add(i)
-            free[e] = st + ops[i]["cost"]
-            fin = free[e] + ops[i]["lat"]
-            end = max(end, fin)
-            order.append(i)
-            for j in succ[i]:
-                ready[j] = max(ready[j], fin + WAKE)
+    def place(before, after, rank_, back):
+        left, start, busy = [len(x) for x in before], [0.0] * n, {}
+        ready = sorted((rank_[i], i) for i in range(n) if not left[i])
+        while ready:
+            i = ready.pop(0)[1]
+            c = ops[i]["cost"]
+            st = max([start[d] + ops[d]["cost"] + (gap(i, d) if back else gap(d, i)) for d in before[i]] + [ops[i]["lat"] if back else 0.0])
+            line = busy.setdefault(ops[i]["eng"], [])
+            k = 0
+            if c:
+                while k < len(line) and line[k][0] < st + c:
+                    st = max(st, line[k][1]); k += 1
+                line.insert(k, (st, st + c))
+            start[i] = st
+            for j in after[i]:
                 left[j] -= 1
-                if not left[j]: cand.setdefault(ops[j]["eng"], []).append(j)
-        return end, order, ready
+                if not left[j]: ready.append((rank_[j], j))
+            ready.sort()
+        return start
 
-    best, known = None, None
-    for k in range(PASSES):
-        end, order, known = schedule(known)
-        if best is None or end < best[0]: best = (end, order)
+    if not ORDER:
+        tail = [0.0] * n
+        for i in range(n - 1, -1, -1):
+            tail[i] = ops[i]["cost"] + max([tail[j] + gap(i, j) for j in succ[i]] + [ops[i]["lat"]])
+        rank_, best = [STAG * ops[i]["grp"] - tail[i] for i in range(n)], None
+        for k in range(PASSES):
+            start = place(pred, succ, rank_, False)
+            end = max(start[i] + ops[i]["cost"] + ops[i]["lat"] for i in range(n))
+            if best is None or end < best[0]: best = (end, start)
+            back = place(succ, pred, [-(start[i] + ops[i]["cost"]) for i in range(n)], True)
+            rank_ = [-(back[i] + ops[i]["cost"]) for i in range(n)]
+        ORDER.extend(sorted(range(n), key=lambda i: (best[1][i], i)))
 
     count, done, waited, ndma = {}, {}, {}, 0
-    for i in best[1]:
+    for i in ORDER:
         o = ops[i]
         e = o["eng"]
         if e == "r":
@@ -407,6 +397,7 @@ def rank_program(g, core, T, topo):
             continue
         need = {}
         for d in o["dep"]:
+            if o.get("adds") and ops[d]["eng"] == "p": continue
             sm, val = done[d]
             need[sm] = max(need.get(sm, 0), val)
         for sm in sorted(need):

@@ -5,13 +5,15 @@ NL = 12 // H
 W = 16 * NL
 R = 3
 RB = 4 if NL > 4 else 8
-ESPLIT, RSPLIT = (0, 2, 4, 6, 7, 8), (0, 2, 4, 6, 8, 10, 12, 14, 16, 17)
+ESPLIT, RSPLIT = (0, 4, 7, 8), (0, 5, 10, 14, 17)
 ON = dict(H="v", F="v", hn="s", h="v", nm="s", B="v", lo="s")
 TWICE = False
 SIGNV = False
+YV = ((1, 0), (2, 1), (3, 0))
 GV = {(1, 0, "y"): 6, (1, 1, "y"): 6}
-CY, VO, SO, PCY, GA = 0.83, 40.0, 55.0, 0.48, 1.55
-WAKE, RLAT, PASSES, STAG = 60.0, 2700.0, 8, 6000.0
+CY, VO, SO, PO, PCY, GA = 0.83, 45.0, 40.0, 60.0, 0.43, 1.3
+WAKE, CROSS, RLAT, LOAD = 120.0, 240.0, 2000.0, 5000.0
+PASSES, STAG = 4, (4000.0, 6000.0, 8000.0)
 BIG = 1.0e9
 NDIFF = 4
 KEY = 512.0
@@ -20,12 +22,12 @@ IDENT = (("ip", 1.0, "bfloat16"), ("im", -1.0, "bfloat16"), ("iH", -31 * KEY, "b
          ("ip8", 8 * KEY, "bfloat16"), ("ip16", 16 * KEY, "bfloat16"), ("iw", 32.0, "bfloat16"), ("iu", 96.0, "bfloat16"),
          ("im63", -63.0, "bfloat16"), ("it1", 38.5, "bfloat16"), ("it2", 77.0, "bfloat16"), ("it3", 115.5, "bfloat16"),
          ("i64", 64.0, "bfloat16"), ("im64", -64.0, "bfloat16"),
-         ("iR", -65 * 64.0, "bfloat16"), ("ia", -1.0 / 128, "bfloat16"), ("ib", 1.0 / 64, "bfloat16"),
+         ("iR", -65 * 64.0, "bfloat16"), ("ia", 1.0 / 128, "bfloat16"), ("ib", -1.0 / 64, "bfloat16"),
          ("iph", 1.0, "float16"), ("i64h", 64.0, "float16"), ("iKh", KEY, "float16"), ("i63h", 63.0, "float16"))
 C0 = 0.0 if SIGNV else 8.0
-FILLS = (("k1", 1.0, None, 0, "bfloat16"), ("kres", 136.0, None, 0, "bfloat16"), ("k28", 28.0, None, 0, "float16"),
-         ("kc1", C0, None, 0, "float16"), ("kc2", C0 + 1.0 / 128 - 272.0 / 128, None, 0, "float16"),
-         ("mk", 1.0, 0, 0.0, "bfloat16"), ("rk", 0.0, 0, BIG, "float32"),
+RES = -65.0 * 64 * 136
+FILLS = (("k1", 1.0, None, 0, "bfloat16"),
+         ("mk", 1.0, 0, 0.0, "bfloat16"), ("rk", -1.0, 0, BIG, "float32"),
          ("rz", 0.0, 15, -1024.0, "bfloat16"), ("rm", 0.0, 15, -1024.0, "bfloat16"), ("rn", 0.0, 15, 1024.0, "bfloat16"))
 SCRATCH = {
     "ct": ("sbuf", [128, 4096], "bfloat16"),
@@ -36,8 +38,9 @@ SCRATCH = {
     "pid": ("sbuf", [128, 1], "int32"), "pbit": ("sbuf", [128, 1], "int32"),
     "modd": ("sbuf", [128, 1], "float32"), "meven": ("sbuf", [128, 1], "float32"),
     "selc": ("sbuf", [128, 160], "bfloat16"), "seld": ("sbuf", [128, 160], "bfloat16"),
-    "krow": ("sbuf", [128, W], "bfloat16"), "k2k": ("sbuf", [128, 192], "float16"),
-    "ku": ("sbuf", [128, 2, W], "float16"), "kt": ("sbuf", [128, 4, W], "bfloat16"),
+    "sely": ("sbuf", [128, 160], "bfloat16"), "selm": ("sbuf", [128, 160], "bfloat16"),
+    "k2k": ("sbuf", [128, 192], "float16"),
+    "ku": ("sbuf", [128, 2, W], "float16"), "kt": ("sbuf", [128, 2, W], "bfloat16"),
     "swp": ("sbuf", [128, 2, 2, 128], "float16"),
     "xf": ("sbuf", [128, 2, 192], "float16"), "xt": ("sbuf", [128, 2, 12, 16], "float16"),
     "le1": ("sbuf", [128, 192], "uint16"), "ls1": ("sbuf", [128, 192], "uint16"), "ls2": ("sbuf", [128, 192], "uint16"),
@@ -50,7 +53,7 @@ for _n, _v, _d in IDENT:
 for _n, _a, _b, _c, _d in FILLS:
     SCRATCH[_n] = ("sbuf", [128, W], _d)
 for _n, _s, _d in (
-        ("v", [NL, 256], "bfloat16"), ("y", [NL, 256], "bfloat16"), ("sg", [NL, 16, 16], "bfloat16"), ("ab", [NL, 16, 16], "bfloat16"),
+        ("v", [NL, 256], "bfloat16"), ("y", [NL, 256], "bfloat16"), ("sg", [NL, 16, 16], "bfloat16"), ("ab", [NL, 16, 16], "bfloat16"), ("dy", [NL, 16, 16], "bfloat16"),
         ("km", [W], "int32"), ("cc", [W], "int32"), ("par", [W], "int32"), ("st", [W], "int32"), ("pos", [W], "bfloat16"),
         ("mx", [W + 16], "bfloat16"), ("mn", [W + 16], "bfloat16"), ("hp", [W], "bfloat16"), ("fp", [W], "bfloat16"),
         ("u", [W], "bfloat16"), ("w", [W], "bfloat16"), ("hs", [W], "bfloat16"), ("hn", [W], "bfloat16"),
@@ -106,12 +109,13 @@ def rank_program(g, core, T, topo):
     def S(n, fn, r=(), w=(), bank=()):
         op("s", SO + n * CY, fn, r, w, bank)
 
-    def P(terms, r=(), w=(), bank=(), start=True, stop=True):
+    def P(terms, r=(), w=(), bank=(), start=True, stop=True, each=False):
         def fn():
-            for i, (o, l, x, n) in enumerate(terms):
-                z = g.tensor.matmul(o, l, x, start and i == 0, stop and i == len(terms) - 1)
+            q = [None if start else 0] + terms + [None if stop else 0]
+            for a, m, c in zip(q, q[1:], q[2:]):
+                if m: z = g.tensor.matmul(m[0], m[1], m[2], each or a is None, each or c is None)
             return z
-        ops[op("p", sum(n for o, l, x, n in terms) * PCY, fn, r, w, bank)]["adds"] = not start
+        ops[op("p", PO + sum(m[3] for m in terms if m) * PCY, fn, r, w, bank)]["adds"] = not start
 
     v, s = g.vector, g.scalar
     ts, tt, scan, act = v.tensor_scalar, v.tensor_tensor, v.tensor_tensor_scan, s.activation
@@ -143,7 +147,7 @@ def rank_program(g, core, T, topo):
 
     dma("y", g.sync, T.en[:], T.enz[:], "lde", ["en"], 2000.0)
     dma("s", g.scalar, T.su[:], T.subs[:], "lds", ["su"], 2000.0)
-    dma("y", g.sync, T.ct[:], T.cont[:], "ldc", ["ct"], 5700.0)
+    dma("y", g.sync, T.ct[:], T.cont[:], "ldc", ["ct"], LOAD)
 
     V(128, lambda: v.memset(T.one[:], 1.0), w=["one"])
     op("g", 140, lambda: g.iota(T.pid[:], [[0, 1]], 0, 1), w=["pid"])
@@ -174,21 +178,20 @@ def rank_program(g, core, T, topo):
         S(192, lambda pn=pn, nm=nm: act(T[nm][:], T[pn][:, 0:12, :], F.Copy), [pn], [nm], [pn])
     send(opp, "ls2", T.ls2[:], T.le1[:], ["ls2"], ["le1"])
     send(opp, "ns2", T.ns2[:], T.ne1[:], ["ns2"], ["ne1"])
-    for n, val in (("selc", 1.0 if SIGNV else 0.5), ("seld", 16.0)):
+    for n, val in (("selc", 1.0 if SIGNV else 0.5), ("seld", 16.0), ("selm", 32.0), ("sely", -16.0)):
         V(80, lambda n=n: v.memset(T[n][:], 0.0), w=[n])
         V(8, lambda n=n, val=val: ts(T[n][:, 15:143:16], T.g8c[:], val, None, A.mult), ["g8c"], [n])
-    op("g", 300, lambda: g.iota(T.krow[:], [[0, NL], [1, 16]], 0, 0, allow_small_or_imprecise_dtypes=True), w=["krow"])
     for n, base, at, val, d in FILLS:
         V(W / 2, lambda n=n, base=base: v.memset(T[n][:], base), w=[n])
         if n in ("rm", "rn"):
             V(W / 4, lambda n=n: v.memset(T[n][:, 1::2], 2.0), w=[n])
         if at is not None:
             V(NL, lambda n=n, at=at, val=val: v.memset(T[n][:, at::16], val), w=[n])
-    for a, val in enumerate((7044.0, 7072.0)):
+    for a, val in enumerate((7028.0, 7056.0)):
         V(W / 2, lambda a=a, val=val: v.memset(T.ku[:, a], val), w=["ku"])
         V(NL, lambda a=a, val=val: v.memset(T.ku[:, a, 15::16], val - 8), w=["ku"])
-    for a, z, val in ((0, 2, 0.0), (2, 3, -192.0), (3, 4, 64.0 * 192 + 2048)):
-        V(W / 2, lambda a=a, z=z, val=val: v.memset(T.kt[:, a:z], val), w=["kt"])
+    for a, val in enumerate((-192.0, 64.0 * 192 + 2048)):
+        V(W / 2, lambda a=a, val=val: v.memset(T.kt[:, a], val), w=["kt"])
     for n in ("mx", "mn"):
         V(16, lambda n=n: v.memset(T[n][:, :, W:W + 16], 0.0), w=[n + "pad"])
 
@@ -221,12 +224,20 @@ def rank_program(g, core, T, topo):
             p, o, xk = T[pn], b("sg")[:, c:c + 2], [("v", h, c), ("v", h, c + 1)]
             turned = lambda m: [(p[:, 0:15, :], m, x[:, c, 16:256], 240), (p[:, 16:31, :], m, x[:, c + 1, 16:256], 240), (p[:, 15::16, :], m, x[:, c:c + 2, 0:16], 64)]
             if SIGNV:
-                for z in turned(T.ip[:]): P([z], xk + ["ip"], [pn], [pn])
+                P(turned(T.ip[:]), xk + ["ip"], [pn], [pn], each=True)
                 V(512, lambda p=p, o=o, c=c: tt(o, x[:, c:c + 2], p[:], A.is_gt), [pn] + xk, [("sg", h, c)], [pn])
             else:
                 P([(p[:], T.ip[:], x[:, c:c + 2], 512)] + turned(T.im[:]), xk + ["ip", "im"], [pn], [pn])
                 S(512, lambda p=p, o=o: act(o, p[:], F.Sign, bias=-0.5), [pn], [("sg", h, c)], [pn])
-        for r in range(0, 16, RB):
+        yv = (t, h) in YV
+        if yv:
+            pn = "pd%d" % (dn[0] % NDIFF); dn[0] += 1
+            p = T[pn]
+            P([(p[:, i:NL * RB:RB, :], T.ip[:], x[:, :, 240:256], W) for i in range(RB)], vk + ["ip"], [pn], [pn], each=True)
+            for r in range(0, 16, RB):
+                V(W * RB, lambda p=p, r=r: tt(b("ab")[:, :, r:r + RB], y[:, :, 16 * r:16 * (r + RB)], p[:, 0:NL * RB, :], A.max), yk + [pn], [("ab", h, r)], [pn])
+            P([(pK, T.sely[:, 15 - m:143 - m], y[:, :, m::16], W) for m in range(16)], yk + ["sely"], [en_ + "K"], [en_], stop=False)
+        for r in range(0, 0 if yv else 16, RB):
             pn = "pd%d" % (dn[0] % NDIFF); dn[0] += 1
             p = T[pn]
             P([(p[:, 0:NL * RB, :], T.ip[:], y[:, :, 16 * r:16 * (r + RB)], W * RB)] + [(p[:, i:NL * RB:RB, :], T.im[:], x[:, :, 240:256], W) for i in range(RB)],
@@ -234,17 +245,16 @@ def rank_program(g, core, T, topo):
             S(W * RB, lambda p=p, o=b("ab")[:, :, r:r + RB]: act(o, p[:, 0:NL * RB, :], F.Abs), [pn], [("ab", h, r)], [pn])
 
         def sums(p, first, sel, z, r, w, bank):
-            P(first, r[0], w, bank, stop=False)
-            for a in range(0, 16, 4):
-                P([(p, sel[:, 15 - m:143 - m], z[:, :, :, m], W) for m in range(a, a + 4)], r[1], w, bank, start=False, stop=a == 12)
-        more = [(pC, T.iph[:], T.kc1[:], W)] if t == 1 else [(pC, T.iph[:], T.kc2[:], W), (pC, T.ia[:], b("nb"), W), (pC, T.ib[:], b("hn"), W)]
-        sums(pC, more, T.selc, b("sg"), (["iph", "kc1", "kc2", "ia", "ib"] + K("nb", "hn"), [("sg", h, c) for c in range(0, NL, 2)] + ["selc"]), [an + "C", an + "T"], [an])
-        sums(pK, [(pK, T.ip[:], T.krow[:], W)], T.seld, b("ab"), (["ip", "krow"], [("ab", h, r) for r in range(0, 16, RB)] + ["seld"]), [en_ + "K"], [en_])
+            P(first + [(p, sel[:, 15 - m:143 - m], z[:, :, :, m], W) for m in range(16)], r[0] + r[1], w, bank, start=not (yv and w == [en_ + "K"]))
+        more = [] if t == 1 else [(pC, T.ia[:], b("nb"), W), (pC, T.ib[:], b("hn"), W)]
+        c0 = C0 if t == 1 else C0 + 2.0
+        sums(pC, more, T.selc, b("sg"), (["ia", "ib"] + K("nb", "hn"), [("sg", h, c) for c in range(0, NL, 2)] + ["selc"]), [an + "C", an + "T"], [an])
+        sums(pK, [], T.selm if yv else T.seld, b("ab"), ([], [("ab", h, r) for r in range(0, 16, RB)] + ["seld", "selm"]), [en_ + "K"], [en_])
         while later: later.pop()()
         grp[0] = h
         V(W, lambda: scan(b("cc"), T.mk[:], pC, 0.0, A.mult, A.add), [an + "C", "mk"], K("cc"), [an])
-        S(W, lambda: act(b("w"), pC, F.Sign, bias=-9.5), [an + "C"], K("w"), [an])
-        S(W, lambda: act(b("u"), pC, F.Sign, bias=5.5 if t == 1 else 6.0 + 1.0 / 256, scale=-1.0), [an + "C"], K("u"), [an])
+        S(W, lambda: act(b("w"), pC, F.Sign, bias=c0 - 9.5), [an + "C"], K("w"), [an])
+        S(W, lambda: act(b("u"), pC, F.Sign, bias=6.0 - 1.0 / 256 - c0, scale=-1.0), [an + "C"], K("u"), [an])
         V(W, lambda: ts(b("par"), b("cc"), 1, None, A.bitwise_and), K("cc"), K("par"))
         for e in range(2):
             V(W / 2, lambda e=e: ts(b("st")[:, e::2], b("par")[:, e::2], -2.0, 2.0 * e - 1.0, A.mult, A.add), K("par"), K("st%d" % e))
@@ -253,8 +263,8 @@ def rank_program(g, core, T, topo):
         V(W, lambda: scan(b("pos"), T.mk[:], b("st"), 0.0, A.mult, A.add), K("st0", "st1") + ["mk"], K("pos"))
         V(W / 2, lambda: scan(b("mx")[:, W - 1::-1], T.rm[:, ::-1], b("pos")[:, ::-1], 0.0, A.add, A.max), K("pos") + ["rm"], K("mx"))
         V(W / 2, lambda: scan(b("mn")[:, W - 1::-1], T.rn[:, ::-1], b("pos")[:, ::-1], 0.0, A.add, A.min), K("pos") + ["rn"], K("mn"))
-        affine("H", W, True, b("hp"), b("pos"), 0.5, 191.75, K("pos"), K("hp"))
-        affine("F", W, True, b("fp"), b("pos"), 1.0 / 16, 136.0 - 15.0 / 32, K("pos"), K("fp"))
+        affine("H", W, True, b("hp"), b("pos"), 0.5, 191.25, K("pos"), K("hp"))
+        affine("F", W, True, b("fp"), b("pos"), 1.0 / 16, 136.0 - 17.0 / 32, K("pos"), K("fp"))
         affine("h", W, True, b("hs"), el, 1.0 / 64, 192.0 - 63.0 / 128, ek, K("hs"))
         affine("h", W, True, b("sh"), el, 1.0, -2048.0, ek, K("sh"))
         mx, mn, it = b("mx"), b("mn"), T["it%d" % t]
@@ -266,30 +276,27 @@ def rank_program(g, core, T, topo):
             P([(reg(an, 0, 2), T.iKh[:], T.ku[:], 2 * W), (pA, T.ip[:], b("hs"), W)] + low(pB) + two(lambda p: [(p, T.iw[:], b("w"), W), (p, T.iu[:], b("u"), W)]),
               K("u") + lowk + ["iKh", "ku", "iw", "iu", "ip"], [an + "C"], [an], stop=False)
         else:
-            P([(pA, T.iKh[:], T.ku[:, 0], W), (pA, T.iw[:], b("w"), W), (pA, T.iu[:], b("u"), W)], K("u", "w") + ["iKh", "ku", "iw", "iu"], [an + "C"], [an], stop=False)
-            P([(pY, T.iKh[:], T.k28[:], W)] + low(pY), lowk + ["iKh", "k28"], [en_ + "Y"], [en_])
-            affine("lo", W, False, b("lo"), pY, 1.0, 0.0, [en_ + "Y"], K("lo"), [en_])
-        P(two(lambda p: [(p, T.ip16[:], b("pos"), W)]), K("pos") + ["ip16"], [an + "C"], [an], start=False, stop=False)
-        P(two(lambda p: [(p, T.im8[:], mx[:, 0:W], W), (p, T.ip8[:], mx[:, 1:W + 1], W), (p[:, 15::16], T.im8[:], mx[:, 16:W + 1:16], 64)]),
-          K("mx") + ["mxpad", "im8", "ip8"], [an + "C"], [an], start=False, stop=False)
-        P(two(lambda p: [(p, T.ip8[:], mn[:, 0:W], W), (p, T.im8[:], mn[:, 1:W + 1], W), (p[:, 15::16], T.ip8[:], mn[:, 16:W + 1:16], 64)]),
-          K("mn") + ["mnpad", "im8", "ip8"], [an + "C"], [an], start=False, stop=False)
+            P([(pA, T.iKh[:], T.ku[:, 0], W), (pA, T.ip[:], b("hs"), W), (pA, T.iw[:], b("w"), W), (pA, T.iu[:], b("u"), W)], K("u", "w", "hs") + ["iKh", "ku", "iw", "iu", "ip"], [an + "C"], [an], stop=False)
+            P([(pY, T.im64[:], b("hs"), W)] + low(pY)[1:3], lowk + ["im64"], [en_ + "Y"], [en_])
+            affine("lo", W, False, b("lo"), pY, 1.0, 64.0 * 192 + 2048 + 38.5 * t, [en_ + "Y"], K("lo"), [en_])
+        P(two(lambda p: [(p, T.ip16[:], b("pos"), W),
+                         (p, T.im8[:], mx[:, 0:W], W), (p, T.ip8[:], mx[:, 1:W + 1], W), (p[:, 15::16], T.im8[:], mx[:, 16:W + 1:16], 64),
+                         (p, T.ip8[:], mn[:, 0:W], W), (p, T.im8[:], mn[:, 1:W + 1], W), (p[:, 15::16], T.ip8[:], mn[:, 16:W + 1:16], 64)]),
+          K("pos", "mx", "mn") + ["ip16", "mxpad", "mnpad", "im8", "ip8"], [an + "C"], [an], start=False, stop=False)
         P(two(lambda p: [(p, T.iH[:], b("hp"), W), (p, T.im8[:], b("fp"), W)]), K("hp", "fp") + ["iH", "im8"], [an + "C"], [an], start=False)
         if TWICE:
             qe, qek = reg(an, 0, 2)[:, 0::2], [an + "C"]
             affine("B", W, False, b("qb"), reg(an, 0, 2)[:, 1::2], 1.0, 0.0, [an + "C"], K("qb0", "qb1"), [an])
         else:
-            qe, qek = reg(an, 1), [an + "Q0", an + "Q1"]
-            for a, n in enumerate(("hs", "lo")):
-                V(W / 2, lambda a=a, n=n: tt(b("qb")[:, a], pA[:, 1::2], b(n)[:, 1::2], A.add), [an + "C"] + K(n), K("qb%d" % a), [an])
-                V(W / 2, lambda a=a, n=n: tt(qe[:, a * W // 2:(a + 1) * W // 2], pA[:, 0::2], b(n)[:, 0::2], A.add), [an + "C"] + K(n), [an + "Q%d" % a], [an])
+            qe, qek = reg(an, 0, 2)[:, 0::2], [an + "C", an + "Q"]
+            V(W / 2, lambda: v.tensor_copy(b("qb")[:, 0], pA[:, 1::2]), [an + "C"], K("qb0"), [an])
+            V(W / 2, lambda: tt(b("qb")[:, 1], pA[:, 1::2], b("lo")[:, 1::2], A.add), [an + "C"] + K("lo"), K("qb1"), [an])
+            V(W / 2, lambda: tt(pB[:, 0::2], pA[:, 0::2], b("lo")[:, 0::2], A.add), [an + "C"] + K("lo"), [an + "Q"], [an])
         V(W, lambda: tt(b("qx"), qe, b("qb"), A.max), qek + K("qb0", "qb1"), K("qx"), [an])
         V(W, lambda: tt(qp[:, :, :, 8:16, 0], qe, b("qb"), A.min), qek + K("qb0", "qb1"), K("qpe"), [an])
         V(W, lambda: ts(qp[:, :, :, 8:16, 1], b("qx"), -16 * KEY, None, A.add), K("qx"), K("qpo"))
         V(14 * NL, lambda: v.tensor_copy(qp[:, :, :, 1:8, :], qp[:, :, :, 9:16, :]), K("qpe", "qpo"), K("qpd"))
         tk = [an + "T"]
-        P([(reg(an, 1, 4), T.ip[:], T.kt[:], 4 * W), (reg(an, 3), T.ip[:], b("hs"), W), (reg(an, 4), T.im64[:], b("hs"), W), (reg(an, 4), T.iph[:], b("sh"), W)],
-          K("hs", "sh") + ["ip", "kt", "im64", "iph", an + "C"], tk, [an], stop=False)
         for a, z in zip(ESPLIT, ESPLIT[1:]):
             for d in range(a, z):
                 V(W, lambda d=d: ts(b("o1")[:, d], qp[:, :, :, 8 - d:16 - d, :], KEY * (d - 4), KEY * (d - 3), A.max, A.min), K("qpe", "qpo") + (K("qpd") if d else []), [("o1", h, d)])
@@ -300,8 +307,10 @@ def rank_program(g, core, T, topo):
         V(W, lambda: ts(b("dl"), b("xx"), 14336.0, None, A.is_ge), K("xx"), K("dl"))
         V(W / 2, lambda: scan(b("ii"), T.mk[:], b("dl"), 0.0, A.mult, A.add), K("dl") + ["mk"], K("ii"))
         V(W / 2, lambda: scan(b("nb")[:, ::-1], T.rz[:, ::-1], b("ii")[:, ::-1], 0.0, A.add, A.max), K("ii") + ["rz"], K("nb"))
-        P([(reg(an, a), m[:], b(n), W) for a in (1, 2) for m, n in ((T.ip8, "dl"), (T.i64, "ii"))], K("dl", "ii") + ["ip8", "i64"], tk, [an], start=False, stop=False)
-        P([(reg(an, a), T.i64[:], b("nb"), W) for a in (3, 4)], K("nb") + ["i64"], tk, [an], start=False)
+        P([(reg(an, 3, 2), T.ip[:], T.kt[:], 2 * W), (reg(an, 3), T.ip[:], b("hs"), W), (reg(an, 4), T.im64[:], b("hs"), W), (reg(an, 4), T.iph[:], b("sh"), W)]
+          + [(reg(an, a), T.i64[:], b("nb"), W) for a in (3, 4)] + [None]
+          + [z for a in (1, 2) for z in ((reg(an, a), T.ip8[:], b("dl"), W), (reg(an, a), T.i64[:], b("ii"), W), None)][:-1],
+          K("hs", "sh", "dl", "ii", "nb") + ["ip", "kt", "im64", "iph", "ip8", "i64", an + "C"], tk, [an])
         V(W, lambda: ts(b("n32"), b("xx"), 2048.0, 32.0, A.is_lt, A.mult), K("xx"), K("n32"))
         V(W, lambda: ts(pY, b("xx"), -8192.0 - 77 * t, 0.0, A.add, A.max), K("xx"), [en_ + "Y"], [en_])
         V(W, lambda: tt(pY, pY, b("n32"), A.add), K("n32"), [en_ + "Y"], [en_])
@@ -313,25 +322,24 @@ def rank_program(g, core, T, topo):
         q2, o2 = b("q2"), b("o2")
         V(2 * W, lambda: v.tensor_copy(q2[:, :, :, 16:32], reg(an, 3, 2)), tk, K("q2b"), [an])
         V(2 * W, lambda: tt(q2[:, :, :, 0:16], reg(an, 1, 2), b("n2"), A.add), tk + K("n2h", "n2l"), K("q2a"), [an])
-        P([(pK, T.iR[:], T.kres[:], W), (pK, T.iR[:], b("nb"), W)], K("nb") + ["iR", "kres"], [en_ + "K", en_ + "X"], [en_], stop=False)
         for a, z in zip(RSPLIT, RSPLIT[1:]):
             for d in range(a, z):
                 d = 16 - d
                 V(W, lambda d=d: ts(o2[:, d], q2[:, :, :, d:d + 16], 64.0 * d, 64.0 * d + 64.0, A.max, A.min), K("q2b") + (K("q2a") if d < 16 else []), [("o2", h, d)])
-            P([(pK, c[:], o2[:, 16 - d, e], W) for d in range(a, z) for e, c in ((0, T.i64h), (1, T.iph))],
-              [("o2", h, 16 - d) for d in range(a, z)] + ["iph", "i64h"], [en_ + "K"], [en_], start=False, stop=z == 17)
+            P([(pK, T.iR[:], b("nb"), W)][:0 if a else 1] + [(pK, c[:], o2[:, 16 - d, e], W) for d in range(a, z) for e, c in ((0, T.i64h), (1, T.iph))],
+              [("o2", h, 16 - d) for d in range(a, z)] + ["iph", "i64h", "iR"] + K("nb"), [en_ + "K", en_ + "X"], [en_], start=a == 0, stop=z == 17)
         if t < R:
             n = t + 1
             ml, mk = b("ml%d" % t), K("ml%d" % t)
-            V(W, lambda: v.tensor_copy(ml, pK), [en_ + "K"], mk, [en_])
+            V(W, lambda: ts(ml, pK, RES, None, A.add), [en_ + "K"], mk, [en_])
             send(nxt, "le%d%d" % (n, h), b("le%d" % n), ml, K("le%d" % n), mk)
             if t + 2 <= R:
-                affine("nm", W, False, b("nm"), pK, 1.0, 0.0, [en_ + "K"], K("nm"), [en_])
+                affine("nm", W, False, b("nm"), pK, 1.0, RES, [en_ + "K"], K("nm"), [en_])
                 send(prv, "ls3%d" % h, b("ls3"), ml, K("ls3"), mk)
                 send(prv, "ns3%d" % h, b("ns3"), b("nm"), K("ns3"), K("nm"))
-            affine("hn", W, True, b("hn"), b("nb"), 0.5, 135.75, K("nb"), K("hn"))
+            affine("hn", W, True, b("hn"), b("nb"), 0.5, 128.25, K("nb"), K("hn"))
         if t >= R - 1:
-            V(W, lambda: ts(b("nh"), pK, -2048.0, None, A.add), [en_ + "K"], K("nh"), [en_])
+            V(W, lambda: ts(b("nh"), pK, RES - 2048.0, None, A.add), [en_ + "K"], K("nh"), [en_])
 
         def result():
             grp[0] = h
@@ -353,7 +361,7 @@ def rank_program(g, core, T, topo):
     succ = [[] for i in range(n)]
     for i in range(n):
         for d in pred[i]: succ[d].append(i)
-    gap = lambda i, j: ops[i]["lat"] + (0.0 if ops[i]["eng"] == "p" and ops[j].get("adds") else WAKE)
+    gap = lambda i, j: ops[i]["lat"] + (CROSS if ops[i]["eng"] != ops[j]["eng"] else 0.0 if ops[j].get("adds") else WAKE)
 
     def place(before, after, rank_, back):
         left, start, busy = [len(x) for x in before], [0.0] * n, {}
@@ -379,13 +387,15 @@ def rank_program(g, core, T, topo):
         tail = [0.0] * n
         for i in range(n - 1, -1, -1):
             tail[i] = ops[i]["cost"] + max([tail[j] + gap(i, j) for j in succ[i]] + [ops[i]["lat"]])
-        rank_, best = [STAG * ops[i]["grp"] - tail[i] for i in range(n)], None
-        for k in range(PASSES):
-            start = place(pred, succ, rank_, False)
-            end = max(start[i] + ops[i]["cost"] + ops[i]["lat"] for i in range(n))
-            if best is None or end < best[0]: best = (end, start)
-            back = place(succ, pred, [-(start[i] + ops[i]["cost"]) for i in range(n)], True)
-            rank_ = [-(back[i] + ops[i]["cost"]) for i in range(n)]
+        best = None
+        for stag in STAG:
+            rank_ = [stag * ops[i]["grp"] - tail[i] for i in range(n)]
+            for k in range(PASSES):
+                start = place(pred, succ, rank_, False)
+                end = max(start[i] + ops[i]["cost"] + ops[i]["lat"] for i in range(n))
+                if best is None or end < best[0]: best = (end, start)
+                back = place(succ, pred, [-(start[i] + ops[i]["cost"]) for i in range(n)], True)
+                rank_ = [-(back[i] + ops[i]["cost"]) for i in range(n)]
         ORDER.extend(sorted(range(n), key=lambda i: (best[1][i], i)))
 
     count, done, waited, ndma = {}, {}, {}, 0

from concourse.mybir import AluOpType as A, ActivationFunctionType as F

H = 2
NL = 12 // H
W = 16 * NL
R = 3
RB = 4 if NL > 4 else 8
ESPLIT, RSPLIT = (0, 4, 7, 8), (0, 5, 10, 14, 17)
ON = dict(H="v", F="v", hn="s", h="v", nm="s", B="v", lo="s")
TWICE = False
SIGNV = False
YV = ((1, 0), (2, 1), (3, 0))
GV = {(1, 0, "y"): 6, (1, 1, "y"): 6}
CY, VO, SO, PO, PCY, GA = 0.83, 45.0, 40.0, 60.0, 0.43, 1.3
WAKE, CROSS, RLAT, LOAD = 120.0, 240.0, 2000.0, 5000.0
PASSES, STAG = 4, (4000.0, 6000.0, 8000.0)
BIG = 1.0e9
NDIFF = 4
KEY = 512.0

IDENT = (("ip", 1.0, "bfloat16"), ("im", -1.0, "bfloat16"), ("iH", -31 * KEY, "bfloat16"), ("im8", -8 * KEY, "bfloat16"),
         ("ip8", 8 * KEY, "bfloat16"), ("ip16", 16 * KEY, "bfloat16"), ("iw", 32.0, "bfloat16"), ("iu", 96.0, "bfloat16"),
         ("im63", -63.0, "bfloat16"), ("it1", 38.5, "bfloat16"), ("it2", 77.0, "bfloat16"), ("it3", 115.5, "bfloat16"),
         ("i64", 64.0, "bfloat16"), ("im64", -64.0, "bfloat16"),
         ("iR", -65 * 64.0, "bfloat16"), ("ia", 1.0 / 128, "bfloat16"), ("ib", -1.0 / 64, "bfloat16"),
         ("iph", 1.0, "float16"), ("i64h", 64.0, "float16"), ("iKh", KEY, "float16"), ("i63h", 63.0, "float16"))
C0 = 0.0 if SIGNV else 8.0
RES = -65.0 * 64 * 136
FILLS = (("k1", 1.0, None, 0, "bfloat16"),
         ("mk", 1.0, 0, 0.0, "bfloat16"), ("rk", -1.0, 0, BIG, "float32"),
         ("rz", 0.0, 15, -1024.0, "bfloat16"), ("rm", 0.0, 15, -1024.0, "bfloat16"), ("rn", 0.0, 15, 1024.0, "bfloat16"))
SCRATCH = {
    "ct": ("sbuf", [128, 4096], "bfloat16"),
    "en": ("sbuf", [128, 192], "int32"), "su": ("sbuf", [128, 192], "int32"),
    "one": ("sbuf", [128, 128], "float32"), "idf": ("sbuf", [128, 128], "float32"),
    "iup": ("sbuf", [128, 128], "float32"), "idn": ("sbuf", [128, 128], "float32"),
    "g8a": ("sbuf", [128, 8], "float32"), "g8b": ("sbuf", [128, 8], "float32"), "g8c": ("sbuf", [128, 8], "float32"),
    "pid": ("sbuf", [128, 1], "int32"), "pbit": ("sbuf", [128, 1], "int32"),
    "modd": ("sbuf", [128, 1], "float32"), "meven": ("sbuf", [128, 1], "float32"),
    "selc": ("sbuf", [128, 160], "bfloat16"), "seld": ("sbuf", [128, 160], "bfloat16"),
    "sely": ("sbuf", [128, 160], "bfloat16"), "selm": ("sbuf", [128, 160], "bfloat16"),
    "k2k": ("sbuf", [128, 192], "float16"),
    "ku": ("sbuf", [128, 2, W], "float16"), "kt": ("sbuf", [128, 2, W], "bfloat16"),
    "swp": ("sbuf", [128, 2, 2, 128], "float16"),
    "xf": ("sbuf", [128, 2, 192], "float16"), "xt": ("sbuf", [128, 2, 12, 16], "float16"),
    "le1": ("sbuf", [128, 192], "uint16"), "ls1": ("sbuf", [128, 192], "uint16"), "ls2": ("sbuf", [128, 192], "uint16"),
    "ne1": ("sbuf", [128, 192], "float32"), "ns1": ("sbuf", [128, 192], "float32"), "ns2": ("sbuf", [128, 192], "float32"),
}
for _n in ["pa0", "pa1", "pe0", "pe1"] + ["pd%d" % _q for _q in range(NDIFF)]:
    SCRATCH[_n] = ("psum", [128, 32, 16] if _n[1] == "d" else [128, 512], "float32")
for _n, _v, _d in IDENT:
    SCRATCH[_n] = ("sbuf", [128, 128], _d)
for _n, _a, _b, _c, _d in FILLS:
    SCRATCH[_n] = ("sbuf", [128, W], _d)
for _n, _s, _d in (
        ("v", [NL, 256], "bfloat16"), ("y", [NL, 256], "bfloat16"), ("sg", [NL, 16, 16], "bfloat16"), ("ab", [NL, 16, 16], "bfloat16"), ("dy", [NL, 16, 16], "bfloat16"),
        ("km", [W], "int32"), ("cc", [W], "int32"), ("par", [W], "int32"), ("st", [W], "int32"), ("pos", [W], "bfloat16"),
        ("mx", [W + 16], "bfloat16"), ("mn", [W + 16], "bfloat16"), ("hp", [W], "bfloat16"), ("fp", [W], "bfloat16"),
        ("u", [W], "bfloat16"), ("w", [W], "bfloat16"), ("hs", [W], "bfloat16"), ("hn", [W], "bfloat16"),
        ("sh", [W], "float16"), ("lo", [W], "float32"),
        ("qb", [2, W // 2], "float32"), ("qx", [W], "float32"), ("qp", [2, NL, 16, 2], "float16"), ("o1", [8, 2, W], "float16"),
        ("ei", [W], "int32"), ("xx", [W], "int32"), ("n32", [W], "bfloat16"),
        ("az", [W], "int32"), ("sf", [W], "int32"), ("b2", [W], "int32"), ("n2", [2, W], "int32"),
        ("dl", [W], "bfloat16"), ("ii", [W], "bfloat16"), ("nb", [W], "bfloat16"),
        ("q2", [2, NL, 32], "float16"), ("o2", [17, 2, W], "float16"),
        ("nm", [W], "float32"), ("nh", [NL, 16], "float16"),
        ("ml1", [W], "uint16"), ("ml2", [W], "uint16"), ("le2", [W], "uint16"), ("le3", [W], "uint16"), ("ls3", [W], "uint16"),
        ("ns3", [W], "float32"),
        ("yo2", [W], "float32"), ("yo3", [W], "float32"), ("ly2", [W], "float32"), ("ly3", [W], "float32")):
    SCRATCH[_n] = ("sbuf", [128, H] + _s, _d)
SEMAPHORES = ["ldc", "lde", "lds", "out", "loc", "vec", "act", "pe", "gp", "ls2", "ns2"] + [
    "%s%d" % (_a, _h) for _a in ("le2", "le3", "ls3", "ns3", "ly2", "ly3") for _h in range(H)]
ORDER = []


def rank_program(g, core, T, topo):
    rank = T.rank_of(core)
    if rank is None:
        return
    N = len(T.cores)
    nxt = T.cores[(rank + 3) % N]
    prv = T.cores[(rank + 7) % N]
    opp = T.cores[(rank + 4) % N]
    queue = {"v": g.vector, "s": g.scalar, "p": g.tensor, "g": g, "y": g.sync}
    engsem = {"v": "vec", "s": "act", "p": "pe", "g": "gp"}
    ops, lastw, rds, banks, grp = [], {}, {}, {}, [0]

    def op(eng, cost, fn, r=(), w=(), bank=(), sem=None, val=0, lat=0.0):
        i = len(ops)
        dep = set()
        for k in r:
            if k in lastw: dep.add(lastw[k])
        for k in w:
            if k in lastw: dep.add(lastw[k])
            dep.update(rds.get(k, ()))
        for b in bank:
            for e, js in banks.setdefault(b, {}).items():
                if e != eng: dep.update(js)
            banks[b][eng] = banks[b].get(eng, [])[-20:] + [i]
        dep.discard(i)
        for k in r: rds.setdefault(k, []).append(i)
        for k in w: lastw[k] = i; rds[k] = []
        ops.append(dict(eng=eng, cost=cost, fn=fn, dep=dep, sem=sem, val=val, lat=lat, grp=grp[0]))
        return i

    def V(n, fn, r=(), w=(), bank=()):
        op("v", VO + n * CY, fn, r, w, bank)

    def S(n, fn, r=(), w=(), bank=()):
        op("s", SO + n * CY, fn, r, w, bank)

    def P(terms, r=(), w=(), bank=(), start=True, stop=True, each=False):
        def fn():
            q = [None if start else 0] + terms + [None if stop else 0]
            for a, m, c in zip(q, q[1:], q[2:]):
                if m: z = g.tensor.matmul(m[0], m[1], m[2], each or a is None, each or c is None)
            return z
        ops[op("p", PO + sum(m[3] for m in terms if m) * PCY, fn, r, w, bank)]["adds"] = not start

    v, s = g.vector, g.scalar
    ts, tt, scan, act = v.tensor_scalar, v.tensor_tensor, v.tensor_tensor_scan, s.activation

    def affine(name, n, half, out, x, scale, bias, r, w, bank=()):
        if ON[name] == "v":
            V(n / 2 if half else n, lambda: ts(out, x, scale, bias, A.mult, A.add), r, w, bank)
        else:
            S(n, lambda: act(out, x, F.Identity, bias=bias, scale=scale), r, w, bank)

    def dma(eng, q, out, in_, sem, w, lat):
        op(eng, 60.0, lambda: [(q.dma_start(out, in_), sem, 16)], (), w, sem=sem, val=16, lat=lat)

    nloc = [0]

    def send(dst, land, out, in_, w, r):
        rid, pid = topo.addr(dst, core)
        m, ne = topo.mask(core, dst), len(topo.engines(core, dst))
        nloc[0] += ne
        i = op("g", 150, lambda: [(g.remote_dma(out, in_, T.sem[land], T.sem.loc, pid, rid, m), None, 0)], r)
        j = op("r", 0, None, (), w, sem=land, val=ne, lat=RLAT)
        ops[j]["dep"].add(i)

    swk = [("swp", j, c) for j in range(2) for c in range(2)] + ["iph", "k2k"]

    def swapped(p, x, n):
        return [(p[:, 0:n, :], T.iph[:], T.k2k[:, 0:16 * n], 16 * n)] + [
            (p[:, j:n:2, :], T.swp[:, j, c, :], x[:, c:n:2, :], max(64, 8 * n)) for j in range(2) for c in range(2)]

    dma("y", g.sync, T.en[:], T.enz[:], "lde", ["en"], 2000.0)
    dma("s", g.scalar, T.su[:], T.subs[:], "lds", ["su"], 2000.0)
    dma("y", g.sync, T.ct[:], T.cont[:], "ldc", ["ct"], LOAD)

    V(128, lambda: v.memset(T.one[:], 1.0), w=["one"])
    op("g", 140, lambda: g.iota(T.pid[:], [[0, 1]], 0, 1), w=["pid"])
    V(1, lambda: ts(T.pbit[:], T.pid[:], 16, None, A.bitwise_and), ["pid"], ["pbit"])
    V(1, lambda: ts(T.modd[:], T.pbit[:], 1.0 / 16, None, A.mult), ["pbit"], ["modd"])
    V(1, lambda: ts(T.meven[:], T.pbit[:], -1.0 / 16, 1.0, A.mult, A.add), ["pbit"], ["meven"])
    for n, base in (("idf", 0), ("iup", 16), ("idn", -16)):
        op("g", 380, lambda n=n, base=base: g.affine_select(T[n][:], T.one[:], [[-1, 128]], A.is_equal, 0.0, base, 1), ["one"], [n])
    for j, c, n in ((0, 0, "idf"), (0, 1, "iup"), (1, 0, "idn"), (1, 1, "idf")):
        m = ("meven", "modd")[j]
        V(128, lambda j=j, c=c, n=n, m=m: ts(T.swp[:, j, c, :], T[n][:], T[m][:], None, A.mult), [n, m], [("swp", j, c)])
    V(8, lambda: v.memset(T.g8a[:], 1.0), w=["g8a"])
    op("g", 190, lambda: g.affine_select(T.g8b[:], T.g8a[:], [[-16, 8]], A.is_ge, 0.0, 0, 1), ["g8a"], ["g8b"])
    op("g", 190, lambda: g.affine_select(T.g8c[:], T.g8b[:], [[16, 8]], A.is_ge, 0.0, 15, -1), ["g8b"], ["g8c"])
    for n, val, d in IDENT:
        if d == "float16":
            V(128, lambda n=n, val=val: ts(T[n][:], T.idf[:], val, None, A.mult), ["idf"], [n])
        else:
            S(128, lambda n=n, val=val: act(T[n][:], T.idf[:], F.Copy, scale=val), ["idf"], [n])
    V(96, lambda: v.memset(T.k2k[:], 2048.0), w=["k2k"])

    for k, (src, l, nm) in enumerate((("en", "le1", "ne1"), ("su", "ls1", "ns1"))):
        pn = "pd%d" % k
        V(192, lambda k=k, src=src: ts(T.xf[:, k], T[src][:], -2048.0, None, A.add), [src], [("xf", k)])
        V(96, lambda k=k: v.transpose(T.xt[:, k], T.xf[:, k]), [("xf", k)], [("xt", k)])
        P(swapped(T[pn], T.xt[:, k], 12), [("xt", k)] + swk, [pn], [pn])
        V(192, lambda pn=pn, l=l: v.tensor_copy(T[l][:], T[pn][:, 0:12, :]), [pn], [l], [pn])
        S(192, lambda pn=pn, nm=nm: act(T[nm][:], T[pn][:, 0:12, :], F.Copy), [pn], [nm], [pn])
    send(opp, "ls2", T.ls2[:], T.le1[:], ["ls2"], ["le1"])
    send(opp, "ns2", T.ns2[:], T.ne1[:], ["ns2"], ["ne1"])
    for n, val in (("selc", 1.0 if SIGNV else 0.5), ("seld", 16.0), ("selm", 32.0), ("sely", -16.0)):
        V(80, lambda n=n: v.memset(T[n][:], 0.0), w=[n])
        V(8, lambda n=n, val=val: ts(T[n][:, 15:143:16], T.g8c[:], val, None, A.mult), ["g8c"], [n])
    for n, base, at, val, d in FILLS:
        V(W / 2, lambda n=n, base=base: v.memset(T[n][:], base), w=[n])
        if n in ("rm", "rn"):
            V(W / 4, lambda n=n: v.memset(T[n][:, 1::2], 2.0), w=[n])
        if at is not None:
            V(NL, lambda n=n, at=at, val=val: v.memset(T[n][:, at::16], val), w=[n])
    for a, val in enumerate((7028.0, 7056.0)):
        V(W / 2, lambda a=a, val=val: v.memset(T.ku[:, a], val), w=["ku"])
        V(NL, lambda a=a, val=val: v.memset(T.ku[:, a, 15::16], val - 8), w=["ku"])
    for a, val in enumerate((-192.0, 64.0 * 192 + 2048)):
        V(W / 2, lambda a=a, val=val: v.memset(T.kt[:, a], val), w=["kt"])
    for n in ("mx", "mn"):
        V(16, lambda n=n: v.memset(T[n][:, :, W:W + 16], 0.0), w=[n + "pad"])

    dn, later = [0], []

    def chunk(t, h):
        grp[0] = h
        b = lambda n: T[n][:, h]
        K = lambda *n: [(x, h) for x in n]
        an, en_ = "pa%d" % ((t * H + h) % 2), "pe%d" % ((t * H + h) % 2)
        reg = lambda p, i, n=1: T[p][:, i * W:(i + n) * W]
        pC, pK, pX, pY = reg(an, 0), reg(en_, 0), reg(en_, 1), reg(en_, 2)
        ws = slice(W * h, W * h + W)
        el, ek = (T.le1[:, ws], ["le1"]) if t == 1 else (b("le%d" % t), K("le%d" % t))
        sl, sk, zn, znk = (T["ls%d" % t][:, ws], ["ls%d" % t], T["ns%d" % t][:, ws], ["ns%d" % t]) if t < 3 else (b("ls3"), K("ls3"), b("ns3"), K("ns3"))

        def gather(n, l, lk):
            for c in range(NL):
                o, x = b(n)[:, c], T.ct[:].indirect(l[:, 16 * c:16 * c + 16])
                if c >= NL - GV.get((t, h, n), 0):
                    V(256 * GA, lambda o=o, x=x: v.tensor_copy(o, x), ["ct"] + lk, [(n, h, c)])
                else:
                    S(256 * GA, lambda o=o, x=x: act(o, x, F.Copy), ["ct"] + lk, [(n, h, c)])
            return [(n, h, c) for c in range(NL)]
        vk = gather("v", el, ek)
        yk = gather("y", sl, sk)
        x, y = b("v"), b("y")
        for c in range(0, NL, 2):
            pn = "pd%d" % (dn[0] % NDIFF); dn[0] += 1
            p, o, xk = T[pn], b("sg")[:, c:c + 2], [("v", h, c), ("v", h, c + 1)]
            turned = lambda m: [(p[:, 0:15, :], m, x[:, c, 16:256], 240), (p[:, 16:31, :], m, x[:, c + 1, 16:256], 240), (p[:, 15::16, :], m, x[:, c:c + 2, 0:16], 64)]
            if SIGNV:
                P(turned(T.ip[:]), xk + ["ip"], [pn], [pn], each=True)
                V(512, lambda p=p, o=o, c=c: tt(o, x[:, c:c + 2], p[:], A.is_gt), [pn] + xk, [("sg", h, c)], [pn])
            else:
                P([(p[:], T.ip[:], x[:, c:c + 2], 512)] + turned(T.im[:]), xk + ["ip", "im"], [pn], [pn])
                S(512, lambda p=p, o=o: act(o, p[:], F.Sign, bias=-0.5), [pn], [("sg", h, c)], [pn])
        yv = (t, h) in YV
        if yv:
            pn = "pd%d" % (dn[0] % NDIFF); dn[0] += 1
            p = T[pn]
            P([(p[:, i:NL * RB:RB, :], T.ip[:], x[:, :, 240:256], W) for i in range(RB)], vk + ["ip"], [pn], [pn], each=True)
            for r in range(0, 16, RB):
                V(W * RB, lambda p=p, r=r: tt(b("ab")[:, :, r:r + RB], y[:, :, 16 * r:16 * (r + RB)], p[:, 0:NL * RB, :], A.max), yk + [pn], [("ab", h, r)], [pn])
            P([(pK, T.sely[:, 15 - m:143 - m], y[:, :, m::16], W) for m in range(16)], yk + ["sely"], [en_ + "K"], [en_], stop=False)
        for r in range(0, 0 if yv else 16, RB):
            pn = "pd%d" % (dn[0] % NDIFF); dn[0] += 1
            p = T[pn]
            P([(p[:, 0:NL * RB, :], T.ip[:], y[:, :, 16 * r:16 * (r + RB)], W * RB)] + [(p[:, i:NL * RB:RB, :], T.im[:], x[:, :, 240:256], W) for i in range(RB)],
              vk + yk + ["ip", "im"], [pn], [pn])
            S(W * RB, lambda p=p, o=b("ab")[:, :, r:r + RB]: act(o, p[:, 0:NL * RB, :], F.Abs), [pn], [("ab", h, r)], [pn])

        def sums(p, first, sel, z, r, w, bank):
            P(first + [(p, sel[:, 15 - m:143 - m], z[:, :, :, m], W) for m in range(16)], r[0] + r[1], w, bank, start=not (yv and w == [en_ + "K"]))
        more = [] if t == 1 else [(pC, T.ia[:], b("nb"), W), (pC, T.ib[:], b("hn"), W)]
        c0 = C0 if t == 1 else C0 + 2.0
        sums(pC, more, T.selc, b("sg"), (["ia", "ib"] + K("nb", "hn"), [("sg", h, c) for c in range(0, NL, 2)] + ["selc"]), [an + "C", an + "T"], [an])
        sums(pK, [], T.selm if yv else T.seld, b("ab"), ([], [("ab", h, r) for r in range(0, 16, RB)] + ["seld", "selm"]), [en_ + "K"], [en_])
        while later: later.pop()()
        grp[0] = h
        V(W, lambda: scan(b("cc"), T.mk[:], pC, 0.0, A.mult, A.add), [an + "C", "mk"], K("cc"), [an])
        S(W, lambda: act(b("w"), pC, F.Sign, bias=c0 - 9.5), [an + "C"], K("w"), [an])
        S(W, lambda: act(b("u"), pC, F.Sign, bias=6.0 - 1.0 / 256 - c0, scale=-1.0), [an + "C"], K("u"), [an])
        V(W, lambda: ts(b("par"), b("cc"), 1, None, A.bitwise_and), K("cc"), K("par"))
        for e in range(2):
            V(W / 2, lambda e=e: ts(b("st")[:, e::2], b("par")[:, e::2], -2.0, 2.0 * e - 1.0, A.mult, A.add), K("par"), K("st%d" % e))
        V(W, lambda: scan(b("km"), T.rk[:], pK, 0.0, A.add, A.min), [en_ + "K", "rk"], K("km"), [en_])
        V(NL, lambda: ts(b("st")[:, 0::16], b("km")[:, 15::16], 15, None, A.bitwise_and), K("km"), K("st0"))
        V(W, lambda: scan(b("pos"), T.mk[:], b("st"), 0.0, A.mult, A.add), K("st0", "st1") + ["mk"], K("pos"))
        V(W / 2, lambda: scan(b("mx")[:, W - 1::-1], T.rm[:, ::-1], b("pos")[:, ::-1], 0.0, A.add, A.max), K("pos") + ["rm"], K("mx"))
        V(W / 2, lambda: scan(b("mn")[:, W - 1::-1], T.rn[:, ::-1], b("pos")[:, ::-1], 0.0, A.add, A.min), K("pos") + ["rn"], K("mn"))
        affine("H", W, True, b("hp"), b("pos"), 0.5, 191.25, K("pos"), K("hp"))
        affine("F", W, True, b("fp"), b("pos"), 1.0 / 16, 136.0 - 17.0 / 32, K("pos"), K("fp"))
        affine("h", W, True, b("hs"), el, 1.0 / 64, 192.0 - 63.0 / 128, ek, K("hs"))
        affine("h", W, True, b("sh"), el, 1.0, -2048.0, ek, K("sh"))
        mx, mn, it = b("mx"), b("mn"), T["it%d" % t]
        pA, pB, qp = reg(an, 0), reg(an, 1), b("qp")
        two = lambda f: [z for p in ((pA, pB) if TWICE else (pA,)) for z in f(p)]
        low = lambda p: [(p, T.im63[:], b("hs"), W), (p, T.iph[:], b("sh"), W), (p, it[:], b("w"), W), (p, it[:], T.k1[:], W)]
        lowk = K("hs", "sh", "w") + ["im63", "iph", "k1", "it%d" % t]
        if TWICE:
            P([(reg(an, 0, 2), T.iKh[:], T.ku[:], 2 * W), (pA, T.ip[:], b("hs"), W)] + low(pB) + two(lambda p: [(p, T.iw[:], b("w"), W), (p, T.iu[:], b("u"), W)]),
              K("u") + lowk + ["iKh", "ku", "iw", "iu", "ip"], [an + "C"], [an], stop=False)
        else:
            P([(pA, T.iKh[:], T.ku[:, 0], W), (pA, T.ip[:], b("hs"), W), (pA, T.iw[:], b("w"), W), (pA, T.iu[:], b("u"), W)], K("u", "w", "hs") + ["iKh", "ku", "iw", "iu", "ip"], [an + "C"], [an], stop=False)
            P([(pY, T.im64[:], b("hs"), W)] + low(pY)[1:3], lowk + ["im64"], [en_ + "Y"], [en_])
            affine("lo", W, False, b("lo"), pY, 1.0, 64.0 * 192 + 2048 + 38.5 * t, [en_ + "Y"], K("lo"), [en_])
        P(two(lambda p: [(p, T.ip16[:], b("pos"), W),
                         (p, T.im8[:], mx[:, 0:W], W), (p, T.ip8[:], mx[:, 1:W + 1], W), (p[:, 15::16], T.im8[:], mx[:, 16:W + 1:16], 64),
                         (p, T.ip8[:], mn[:, 0:W], W), (p, T.im8[:], mn[:, 1:W + 1], W), (p[:, 15::16], T.ip8[:], mn[:, 16:W + 1:16], 64)]),
          K("pos", "mx", "mn") + ["ip16", "mxpad", "mnpad", "im8", "ip8"], [an + "C"], [an], start=False, stop=False)
        P(two(lambda p: [(p, T.iH[:], b("hp"), W), (p, T.im8[:], b("fp"), W)]), K("hp", "fp") + ["iH", "im8"], [an + "C"], [an], start=False)
        if TWICE:
            qe, qek = reg(an, 0, 2)[:, 0::2], [an + "C"]
            affine("B", W, False, b("qb"), reg(an, 0, 2)[:, 1::2], 1.0, 0.0, [an + "C"], K("qb0", "qb1"), [an])
        else:
            qe, qek = reg(an, 0, 2)[:, 0::2], [an + "C", an + "Q"]
            V(W / 2, lambda: v.tensor_copy(b("qb")[:, 0], pA[:, 1::2]), [an + "C"], K("qb0"), [an])
            V(W / 2, lambda: tt(b("qb")[:, 1], pA[:, 1::2], b("lo")[:, 1::2], A.add), [an + "C"] + K("lo"), K("qb1"), [an])
            V(W / 2, lambda: tt(pB[:, 0::2], pA[:, 0::2], b("lo")[:, 0::2], A.add), [an + "C"] + K("lo"), [an + "Q"], [an])
        V(W, lambda: tt(b("qx"), qe, b("qb"), A.max), qek + K("qb0", "qb1"), K("qx"), [an])
        V(W, lambda: tt(qp[:, :, :, 8:16, 0], qe, b("qb"), A.min), qek + K("qb0", "qb1"), K("qpe"), [an])
        V(W, lambda: ts(qp[:, :, :, 8:16, 1], b("qx"), -16 * KEY, None, A.add), K("qx"), K("qpo"))
        V(14 * NL, lambda: v.tensor_copy(qp[:, :, :, 1:8, :], qp[:, :, :, 9:16, :]), K("qpe", "qpo"), K("qpd"))
        tk = [an + "T"]
        for a, z in zip(ESPLIT, ESPLIT[1:]):
            for d in range(a, z):
                V(W, lambda d=d: ts(b("o1")[:, d], qp[:, :, :, 8 - d:16 - d, :], KEY * (d - 4), KEY * (d - 3), A.max, A.min), K("qpe", "qpo") + (K("qpd") if d else []), [("o1", h, d)])
            P([(pX, c[:], b("o1")[:, d, e], W) for d in range(a, z) for e, c in ((0, T.i63h), (1, T.iph))], [("o1", h, d) for d in range(a, z)] + ["i63h", "iph"],
              [en_ + "X", en_ + "Y"], [en_], start=a == 0, stop=z == 8)
        V(W, lambda: v.tensor_copy(b("ei"), pX), [en_ + "X"], K("ei"), [en_])
        V(W, lambda: ts(b("xx"), b("ei"), 32767, None, A.bitwise_and), K("ei"), K("xx"))
        V(W, lambda: ts(b("dl"), b("xx"), 14336.0, None, A.is_ge), K("xx"), K("dl"))
        V(W / 2, lambda: scan(b("ii"), T.mk[:], b("dl"), 0.0, A.mult, A.add), K("dl") + ["mk"], K("ii"))
        V(W / 2, lambda: scan(b("nb")[:, ::-1], T.rz[:, ::-1], b("ii")[:, ::-1], 0.0, A.add, A.max), K("ii") + ["rz"], K("nb"))
        P([(reg(an, 3, 2), T.ip[:], T.kt[:], 2 * W), (reg(an, 3), T.ip[:], b("hs"), W), (reg(an, 4), T.im64[:], b("hs"), W), (reg(an, 4), T.iph[:], b("sh"), W)]
          + [(reg(an, a), T.i64[:], b("nb"), W) for a in (3, 4)] + [None]
          + [z for a in (1, 2) for z in ((reg(an, a), T.ip8[:], b("dl"), W), (reg(an, a), T.i64[:], b("ii"), W), None)][:-1],
          K("hs", "sh", "dl", "ii", "nb") + ["ip", "kt", "im64", "iph", "ip8", "i64", an + "C"], tk, [an])
        V(W, lambda: ts(b("n32"), b("xx"), 2048.0, 32.0, A.is_lt, A.mult), K("xx"), K("n32"))
        V(W, lambda: ts(pY, b("xx"), -8192.0 - 77 * t, 0.0, A.add, A.max), K("xx"), [en_ + "Y"], [en_])
        V(W, lambda: tt(pY, pY, b("n32"), A.add), K("n32"), [en_ + "Y"], [en_])
        V(W, lambda: tt(b("az"), pY, zn, A.mult), [en_ + "Y"] + znk, K("az"), [en_])
        V(W, lambda: ts(b("sf"), b("az"), 5, 4095, A.arith_shift_right, A.bitwise_and), K("az"), K("sf"))
        V(W, lambda: tt(b("b2"), pX, b("sf"), A.add), [en_ + "X"] + K("sf"), K("b2"), [en_])
        V(W, lambda: ts(b("n2")[:, 0], b("b2"), 6, 63, A.arith_shift_right, A.bitwise_and), K("b2"), K("n2h"))
        V(W, lambda: ts(b("n2")[:, 1], b("b2"), 63, None, A.bitwise_and), K("b2"), K("n2l"))
        q2, o2 = b("q2"), b("o2")
        V(2 * W, lambda: v.tensor_copy(q2[:, :, :, 16:32], reg(an, 3, 2)), tk, K("q2b"), [an])
        V(2 * W, lambda: tt(q2[:, :, :, 0:16], reg(an, 1, 2), b("n2"), A.add), tk + K("n2h", "n2l"), K("q2a"), [an])
        for a, z in zip(RSPLIT, RSPLIT[1:]):
            for d in range(a, z):
                d = 16 - d
                V(W, lambda d=d: ts(o2[:, d], q2[:, :, :, d:d + 16], 64.0 * d, 64.0 * d + 64.0, A.max, A.min), K("q2b") + (K("q2a") if d < 16 else []), [("o2", h, d)])
            P([(pK, T.iR[:], b("nb"), W)][:0 if a else 1] + [(pK, c[:], o2[:, 16 - d, e], W) for d in range(a, z) for e, c in ((0, T.i64h), (1, T.iph))],
              [("o2", h, 16 - d) for d in range(a, z)] + ["iph", "i64h", "iR"] + K("nb"), [en_ + "K", en_ + "X"], [en_], start=a == 0, stop=z == 17)
        if t < R:
            n = t + 1
            ml, mk = b("ml%d" % t), K("ml%d" % t)
            V(W, lambda: ts(ml, pK, RES, None, A.add), [en_ + "K"], mk, [en_])
            send(nxt, "le%d%d" % (n, h), b("le%d" % n), ml, K("le%d" % n), mk)
            if t + 2 <= R:
                affine("nm", W, False, b("nm"), pK, 1.0, RES, [en_ + "K"], K("nm"), [en_])
                send(prv, "ls3%d" % h, b("ls3"), ml, K("ls3"), mk)
                send(prv, "ns3%d" % h, b("ns3"), b("nm"), K("ns3"), K("nm"))
            affine("hn", W, True, b("hn"), b("nb"), 0.5, 128.25, K("nb"), K("hn"))
        if t >= R - 1:
            V(W, lambda: ts(b("nh"), pK, RES - 2048.0, None, A.add), [en_ + "K"], K("nh"), [en_])

        def result():
            grp[0] = h
            pn = "pd%d" % (dn[0] % NDIFF); dn[0] += 1
            P(swapped(T[pn], b("nh"), NL), K("nh") + swk, [pn], [pn])
            V(W, lambda: v.transpose(b("yo%d" % t), T[pn][:, 0:NL, :]), [pn], K("yo%d" % t), [pn])
            send(nxt if t == R else prv, "ly%d%d" % (t, h), b("ly%d" % t), b("yo%d" % t), K("ly%d" % t), K("yo%d" % t))
            y_ = T.yenz if t == R else T.ysub
            op("y", 60, lambda: [(g.sync.dma_start(y_[:, ws], b("ly%d" % t)), "out", 16)], K("ly%d" % t), lat=2000.0)
        if t >= R - 1: later.append(result)

    for t in range(1, R + 1):
        for h in range(H):
            chunk(t, h)
    for f in later: f()

    n = len(ops)
    pred = [sorted(o["dep"]) for o in ops]
    succ = [[] for i in range(n)]
    for i in range(n):
        for d in pred[i]: succ[d].append(i)
    gap = lambda i, j: ops[i]["lat"] + (CROSS if ops[i]["eng"] != ops[j]["eng"] else 0.0 if ops[j].get("adds") else WAKE)

    def place(before, after, rank_, back):
        left, start, busy = [len(x) for x in before], [0.0] * n, {}
        ready = sorted((rank_[i], i) for i in range(n) if not left[i])
        while ready:
            i = ready.pop(0)[1]
            c = ops[i]["cost"]
            st = max([start[d] + ops[d]["cost"] + (gap(i, d) if back else gap(d, i)) for d in before[i]] + [ops[i]["lat"] if back else 0.0])
            line = busy.setdefault(ops[i]["eng"], [])
            k = 0
            if c:
                while k < len(line) and line[k][0] < st + c:
                    st = max(st, line[k][1]); k += 1
                line.insert(k, (st, st + c))
            start[i] = st
            for j in after[i]:
                left[j] -= 1
                if not left[j]: ready.append((rank_[j], j))
            ready.sort()
        return start

    if not ORDER:
        tail = [0.0] * n
        for i in range(n - 1, -1, -1):
            tail[i] = ops[i]["cost"] + max([tail[j] + gap(i, j) for j in succ[i]] + [ops[i]["lat"]])
        best = None
        for stag in STAG:
            rank_ = [stag * ops[i]["grp"] - tail[i] for i in range(n)]
            for k in range(PASSES):
                start = place(pred, succ, rank_, False)
                end = max(start[i] + ops[i]["cost"] + ops[i]["lat"] for i in range(n))
                if best is None or end < best[0]: best = (end, start)
                back = place(succ, pred, [-(start[i] + ops[i]["cost"]) for i in range(n)], True)
                rank_ = [-(back[i] + ops[i]["cost"]) for i in range(n)]
        ORDER.extend(sorted(range(n), key=lambda i: (best[1][i], i)))

    count, done, waited, ndma = {}, {}, {}, 0
    for i in ORDER:
        o = ops[i]
        e = o["eng"]
        if e == "r":
            done[i] = (o["sem"], o["val"])
            continue
        need = {}
        for d in o["dep"]:
            if o.get("adds") and ops[d]["eng"] == "p": continue
            sm, val = done[d]
            need[sm] = max(need.get(sm, 0), val)
        for sm in sorted(need):
            if waited.get((e, sm), 0) < need[sm]:
                queue[e].wait_ge(T.sem[sm], need[sm])
                waited[(e, sm)] = need[sm]
        x = o["fn"]()
        if isinstance(x, list):
            ins, sm, inc = x[0]
            if sm is not None:
                ins.then_inc(T.sem[sm], inc)
                if sm == "out": ndma += inc
            done[i] = (sm, o["val"]) if sm else ("loc", 0)
        else:
            sm = engsem[e]
            x.then_inc(T.sem[sm], 1)
            count[sm] = count.get(sm, 0) + 1
            done[i] = (sm, count[sm])
    g.sync.wait_ge(T.sem.out, ndma)
    g.wait_ge(T.sem.loc, nloc[0])
    for sm in count:
        g.wait_ge(T.sem[sm], count[sm])
